import numpy as np, ml_dtypes
CORES = [16,17,18,19,32,33,34,35]
N = 8
BF = ml_dtypes.bfloat16
S, A, L, M, R, D = 128, 32, 32, 2, 32, 16
def steps(nx, sy):
    g = np.arange(8); s = np.zeros(8, np.int64); place = np.zeros((N * L, 8), np.int64); cnt = np.zeros((N * L, 8), np.int64)
    for i in range(N * L):
        place[i] = sy[i // L, :, i % L].astype(np.int64) * S + s
        v = nx[i // L, g, place[i]].astype(np.int64)
        s = v % S; cnt[i] = v // S
    return place, cnt
def counts(rng, uneven=False):
    k = np.argsort(rng.random((N, 8, S, A)), -1)
    w = rng.integers(0, 2, k.shape) * M if uneven else rng.integers(0, M + 1, k.shape)
    return np.ascontiguousarray(np.where(k <= M, k, w).transpose(0, 1, 3, 2))
def perms(rng):
    return np.argsort(rng.random((N, 8, A, S)), -1)
def bounds(rng):
    e = np.zeros((8, N + 1), np.int64)
    e[:, 1:N] = np.arange(1, N) * R + rng.integers(-D, D + 1, (8, N - 1)); e[:, N] = N * R - rng.integers(0, D + 1, 8)
    e[0, N] = N * R - D; e[7, N] = N * R
    return e
def draw(rng, to, ct, e, burst=False):
    n = (e[:, 1:] - e[:, :-1])[:, :, None]
    k = (np.arange(L * M) - M * rng.integers(0, L, (8, N, 1))) % (L * M) if burst else np.argsort(rng.random((8, N, L * M)), -1)
    c = np.sum((k < n).reshape(8, N, L, M), axis=-1)
    g = np.arange(8); s = np.zeros(8, np.int64); sy = np.zeros((N, 8, L), np.int32)
    for i in range(N * L):
        q = i // L; ok = ct[q][g, :, s] == c[:, q, i % L][:, None]
        a = np.argmax(np.where(ok, rng.random((8, A)), -1.0), axis=1)
        sy[q, :, i % L] = a; s = to[q][g, a, s]
    return {"nx": (ct * S + to).reshape(N, 8, A * S).astype(np.int32), "em": rng.integers(0, 64 ** M, (N, 8, A * S)).astype(np.int32), "sy": sy}
def setup_inputs(rng):
    to = np.where(rng.random((N, 8, A, 1)) < 0.125, rng.integers(0, S, (N, 8, A, S)), perms(rng))
    return draw(rng, to, counts(rng), bounds(rng))
def setup_inputs_edge(rng):
    e = bounds(rng); g = np.arange(8)[:, None]; r = np.arange(1, N)[None, :]
    e[:, 1:N] = r * R + D * np.where(g % 2 == 0, 1 - 2 * ((r + g // 2) % 2), 1 - 2 * (g // 2 % 2)); e[:, N] = N * R - D * (np.arange(8) // 4)
    return draw(rng, perms(rng), counts(rng), e)
def setup_inputs_even(rng):
    e = bounds(rng); e[:] = np.arange(N + 1) * R
    return draw(rng, perms(rng), counts(rng), e)
def setup_inputs_merge(rng):
    kind = (np.argsort(rng.random((N, 8, A)), -1) % 4)[:, :, :, None]; h = (N, 8, A, 1); s = np.arange(S)
    one = np.where(rng.random(h) < 0.5, rng.integers(0, 2, h) * (S - 1), rng.integers(0, S, h))
    to = np.where(kind == 0, one, np.where(kind == 1, s, np.where(kind == 2, (s + 1) % S, rng.integers(0, S, (N, 8, A, S)))))
    return draw(rng, to, counts(rng), bounds(rng))
def setup_inputs_spread(rng):
    to = np.minimum(np.floor(S * rng.random((N, 8, A, S)) ** 6), S - 1).astype(np.int64)
    d = draw(rng, to, counts(rng, True), bounds(rng), True)
    h = (N, 8, A * S); d["em"] = (d["em"] >> np.where(rng.random(h) < 0.5, rng.integers(0, 6 * M, h), 0)).astype(np.int32)
    return d
def check_inputs(d):
    bad = []
    for k, top in (("nx", (M + 1) * S), ("em", 64 ** M), ("sy", A)):
        if d[k].min() < 0 or d[k].max() >= top: bad.append("range of " + k)
    if bad: return bad
    place, cnt = steps(d["nx"], d["sy"])
    off = np.add.accumulate(cnt, 0)[L - 1::L] - R * np.arange(1, N + 1)[:, None]
    if (np.abs(off) > D).any(): bad.append("running totals")
    if (off[-1] > 0).any(): bad.append("whole total")
    return bad
def reference(nx, em, sy):
    place, cnt = steps(nx, sy); g = np.broadcast_to(np.arange(8), (N * L, 8)); r = (np.arange(N * L) // L)[:, None]
    e = em[r, g, place].astype(np.int64); beg = np.add.accumulate(cnt, 0) - cnt
    z = np.full((8, N * R), -1, np.int64)
    for m in range(M):
        on = cnt > m
        z[g[on], beg[on] + m] = ((e >> (6 * m)) & 63)[on]
    return {"y": np.ascontiguousarray(z.reshape(8, N, R).transpose(1, 0, 2)).astype(np.float32)}

@@ -1,0 +1,480 @@
+from concourse.bass import DstId, RemoteDMATransfer
+from concourse.mybir import dt, AluOpType, AxisListType, ActivationFunctionType
+
+_BUF = {
+    "int32": "PI:1 CI:4 SYI:2x32 X:2x128 XA:2x128 EM:2x128 EI0:2x128",
+    "uint16": "LST:3x64 LA:32 LB:16 LC:8 LL:64 X1:16 X4:16 OFP:4 OF2:2",
+    "float32": "PF:1 CF:4 RI:128 IR:128 GC:128 J16:128 KEY:128 MG:4 MS:16 S0:16 Q1:1 CORR:1 MU:1 M1:1 K1:1 KP:1 RA:1 S1:1 "
+               "SD0:128 SD1:128 KC:4 EMF:2x128 EA:2x128 QI:2 ST:2 TA:2x128 NV:4 OWN:1 BEG:1 A1:1 B1:1 U:2 U1:2 U2:2 U3:2 "
+               "U4:2 Y1:32",
+    "bfloat16": "R:128 XR:128 BRR:192 DG:8x128 ZB:128 G4:128 R3:128 BO:128 RB:8x128 ONE:128 IO1:64 TU:128 TRI:128 "
+                "SYB:2x32 XT:2x128 XS:2x128 XB:2x128 EB:2x2x128 SG:2x2x128 SEL:4x2x8 LS:4x2x64 LSH:2x2x64 YB:16x64 T3:128 "
+                "T1:128 WH:1024 HH:1024 W3:1024 W2:1024 W1:1024 W0:1024 QM:512 HM:256 MM:128 SD:128 SCA:512 SCB:256 "
+                "SCC:128 SCM:128 FB:896 M6:128 PW:128 EW:512 MK:64 RST:64 GV:64 SCN:64 FL:64 INC:64 POS:4 OH:4x64 OD:64 "
+                "NB:64 F:192",
+}
+SCRATCH = {n: ("sbuf", [128] + [int(x) for x in d.split("x")], t)
+           for t, l in _BUF.items() for n, d in (w.split(":") for w in l.split())}
+for _n, _d in (("PSA", [512]), ("PSL", [64, 8]), ("PWA", [512]), ("PWB", [512]), ("PTT", [4, 128]), ("PE0", [512]),
+               ("PE1", [512]), ("PSO", [512])):
+    SCRATCH[_n] = ("psum", [128] + _d, "float32")
+SEMAPHORES = (["v", "s", "t", "q", "dsy", "dx", "dxs", "dem", "dy", "ls"]
+              + [p + "_%d" % j for p in ("e1", "en", "ev") for j in range(8)])
+
+
+def rank_program(g, core, T, topo):
+    rank = T.rank_of(core)
+    if rank is None:
+        return
+    OP, ACT, AX = AluOpType, ActivationFunctionType, AxisListType
+    NR = len(T.cores)
+    mine = [r for r, c in enumerate(T.cores) if topo.chip(c) == topo.chip(core)]
+    j = mine.index(rank)
+    first = mine[0] == 0
+    Q = {"v": g.vector, "s": g.scalar, "t": g.tensor, "q": g, "y": g.sync}
+    cnt = {"v": 0, "s": 0, "t": 0, "q": 0}
+    seen = {}
+    V, S, PE = g.vector, g.scalar, g.tensor
+
+    def need(e, *toks):
+        for sem, n in toks:
+            if seen.get((e, sem), 0) < n:
+                Q[e].wait_ge(T.sem[sem], n)
+                seen[(e, sem)] = n
+
+    def did(e, ins):
+        cnt[e] += 1
+        ins.then_inc(T.sem[e], 1)
+        return (e, cnt[e])
+
+    def ts(out, in0, s1, op0, s2=None, op1=None):
+        if op1 is None:
+            return did("v", V.tensor_scalar(out, in0, s1, None, op0))
+        return did("v", V.tensor_scalar(out, in0, s1, s2, op0, op1))
+
+    def tt(out, in0, in1, op):
+        return did("v", V.tensor_tensor(out, in0, in1, op))
+
+    def vcopy(out, in_):
+        return did("v", V.tensor_copy(out, in_))
+
+    def fill(ap, x):
+        return did("v", V.memset(ap, x))
+
+    def scan(out, d0, d1, o0, o1):
+        return did("v", V.tensor_tensor_scan(out, d0, d1, 0.0, o0, o1))
+
+    def act(out, in_, func, **k):
+        return did("s", S.activation(out, in_, func, **k))
+
+    def scopy(out, in_, **k):
+        return act(out, in_, ACT.Copy, **k)
+
+    def mm(out, lhsT, rhs, start=True, stop=True):
+        return did("t", PE.matmul(out, lhsT, rhs, start, stop))
+
+    def iota(out, pattern, cm=0, base=0):
+        return did("q", g.iota(out, pattern, base, cm, allow_small_or_imprecise_dtypes=True))
+
+    def same(r, r2):
+        return topo.chip(T.cores[r]) == topo.chip(T.cores[r2])
+
+    def plan(r, dsts):
+        near, far = [d for d in dsts if same(r, d)], [d for d in dsts if not same(r, d)]
+        p = []
+        if near:
+            es = topo.engines(T.cores[r], T.cores[near[0]])
+            if far or r + 1 == NR:
+                other = [d for d in range(NR) if not same(r, d)][0]
+                es = [e for e in es if e not in topo.engines(T.cores[r], T.cores[other])]
+            p.append((near, es))
+        if far:
+            p.append((far, topo.engines(T.cores[r], T.cores[far[0]])))
+        return p
+
+    def later(r):
+        return list(range(NR - 1, r, -1))
+
+    def beside(r):
+        return [x for x in range(NR) if abs(x - r) == 1]
+
+    def arrive(kind, r):
+        dsts = beside(r) if kind == "ev" else later(r)
+        return ("%s_%d" % (kind, r), [len(es) for ds, es in plan(r, dsts) if rank in ds][0])
+    sent = [0]
+
+    def send(kind, dsts, src_, where):
+        trs = []
+        for ds, es in plan(rank, dsts):
+            adr = [topo.addr(T.cores[d]) for d in ds]
+            trs.append(RemoteDMATransfer(dst_ids=[DstId(rid=x[0], pnc=x[1]) for x in adr],
+                                         dma_engine_mask=sum(1 << e for e in es),
+                                         remote_sem=T.sem["%s_%d" % (kind, rank)], srcs=[src_], dsts=[where(d) for d in ds]))
+            sent[0] += len(es)
+        g.remote_dma_fused(trs, local_sem=T.sem.ls)
+
+    g.sync.dma_start(T.X[:, 0, :], T.nx[0:4, :]).then_inc(T.sem.dx, 16)
+    S.dma_start(T.X[:, 1, :], T.nx[4:8, :]).then_inc(T.sem.dxs, 16)
+    g.sync.dma_start(T.SYI[0:4, 0, :], T.sy[0:4, :]).then_inc(T.sem.dsy, 16)
+    S.dma_start(T.SYI[0:4, 1, :], T.sy[4:8, :]).then_inc(T.sem.dsy, 16)
+    g.sync.dma_start(T.EM[:, 0, :], T.em[0:4, :]).then_inc(T.sem.dem, 16)
+    g.sync.dma_start(T.EM[:, 1, :], T.em[4:8, :]).then_inc(T.sem.dem, 16)
+    dsy, dx, dxs, dem = ("dsy", 32), ("dx", 16), ("dxs", 16), ("dem", 32)
+
+    k_pi = did("q", g.iota(T.PI[:], [[0, 1]], 0, 1))
+    k_gc = iota(T.GC[:], [[1, 8], [0, 16]])
+    k_ir = iota(T.IR[:], [[1, 128]])
+    k_ri = iota(T.RI[0:4, :], [[1, 4], [0, 32]])
+    k_pf = iota(T.PF[:], [[0, 1]], 1)
+    k_j16 = iota(T.J16[:], [[0, 8], [1, 16]])
+    k_br = iota(T.BRR[0:1, :], [[0, 6], [128, 4], [0, 8]])
+    k_xr = iota(T.XR[:], [[1, 128]])
+    k_key = iota(T.KEY[:], [[0, 8], [1, 2], [2, 8]])
+    k_kc = iota(T.KC[:], [[128, 4]])
+
+    c_ls0 = fill(T.LS[:], 0.0)
+    need("v", k_pi)
+    for i, (x, op) in enumerate(((15, OP.bitwise_and), (31, OP.bitwise_and), (5, OP.arith_shift_right),
+                                 (4, OP.arith_shift_right))):
+        a = ts(T.CI[:, i:i + 1], T.PI[:], x, op)
+    need("v", a)
+    c_cf = vcopy(T.CF[:], T.CI[:])
+    q_, a_, gt_, gp_ = [T.CF[:, i:i + 1] for i in range(4)]
+    need("v", c_cf, k_gc)
+    c_bo = ts(T.BO[:], T.GC[:], gp_, OP.is_equal)
+    c_mu = ts(T.MU[:], q_, 8.0, OP.is_ge)
+    ts(T.M1[:], q_, 8.0, OP.is_lt)
+    need("v", k_ir)
+    c_ms = ts(T.MS[:], T.IR[:, 0:16], q_, OP.is_equal)
+    c_mg = ts(T.MG[:], T.IR[:, 0:4], gt_, OP.is_equal)
+    c_one = fill(T.ONE[:], 1.0)
+    need("v", c_mu)
+    c_k1 = ts(T.K1[:], T.MU[:], -15.0, OP.mult)
+    need("s", c_bo, c_ms)
+    for b in range(8):
+        s_rb = scopy(T.RB[:, b, :], T.BO[:], scale=T.MS[:, b:b + 1])
+    need("v", c_k1)
+    c_kp = ts(T.KP[:], q_, 2.0, OP.mult, T.K1[:], OP.add)
+    need("v", k_ri, k_pf)
+    c_r = ts(T.R[0:4, :], T.RI[0:4, :], T.PF[0:4, :], OP.is_equal)
+    need("v", dsy)
+    c_syb = vcopy(T.SYB[0:4], T.SYI[0:4])
+    need("t", c_syb, c_r)
+    for k in range(4):
+        p_rep = mm(T.PSA[:, 16 * k:16 * k + 16], T.R[0:4, :], T.SYB[0:4, :, k:32:4])
+    need("v", dx, dxs)
+    a = ts(T.XA[:], T.X[:], 127, OP.bitwise_and)
+    need("v", p_rep)
+    c_sel = ts(T.SEL[:], T.PSA[:, 0:64], a_, OP.is_equal)
+    need("v", a)
+    c_xt = vcopy(T.XT[:], T.XA[:])
+    need("s", c_sel, c_mg, c_ls0)
+    for gg in range(4):
+        s_ls = scopy(T.LS[:, :, :, 16 * gg:16 * gg + 8], T.SEL[:], scale=T.MG[:, gg:gg + 1])
+    need("t", s_ls, c_xt)
+    for t in range(2):
+        p_t3 = mm(T.PSA[64 * t:64 * t + 64, 128:256], T.LS[:, 3, t, :], T.XT[:, t, :])
+    need("s", p_t3)
+    s_t3 = scopy(T.T3[:], T.PSA[:, 128:256])
+    need("v", c_xt, c_mg)
+    c_yb = []
+    for t in range(2):
+        for gg in range(4):
+            a = ts(T.YB[:, 8 * t:8 * t + 8, 16 * gg:16 * gg + 16], T.XT[:, t, :], T.MG[:, gg:gg + 1], OP.mult)
+        c_yb.append(a)
+
+    def lists(t):
+        need("t", c_one, k_br)
+        mm(T.PSL[64 * t:64 * t + 64, 0:24, :], T.ONE[0:1, 0:64], T.BRR[0:1, :], True, False)
+        need("t", c_yb[t], c_sel)
+        for c in range(8):
+            x = mm(T.PSL[64 * t:64 * t + 64, 0:24, c], T.YB[:, 8 * t + c, :], T.SEL[:, 0:3, t, :], False, c == 7)
+        return x
+    lists(0)
+    need("t", s_t3, s_rb)
+    for b in range(4):
+        p_wb = mm(T.PWB[:, 128 * b:128 * b + 128], T.RB[:, 4 + b, :], T.T3[:])
+    for b in range(3):
+        p_wa = mm(T.PWA[:, 128 * b:128 * b + 128], T.RB[:, b, :], T.T3[:])
+    p_w3 = mm(T.PSO[:, 0:128], T.RB[:, 3, :], T.T3[:])
+    p_l = lists(1)
+    for t in range(2):
+        p_t1 = mm(T.PSA[64 * t:64 * t + 64, 320:448], T.LS[:, 1, t, :], T.XT[:, t, :])
+    need("s", p_wb)
+    s_w = scopy(T.W3[:, 512:1024], T.PWB[:])
+    need("s", p_w3)
+    s_w3 = scopy(T.W3[:, 384:512], T.PSO[:, 0:128])
+    need("s", p_t1)
+    s_t1 = scopy(T.T1[:], T.PSA[:, 320:448])
+    need("v", k_j16)
+    a = ts(T.Q1[:], q_, 1.0, OP.add)
+    x0 = ts(T.SD0[:], T.J16[:], q_, OP.is_equal, -65536.0, OP.mult)
+    need("v", a)
+    x1 = ts(T.SD1[:], T.J16[:], T.Q1[:], OP.is_equal, 128.0, OP.mult)
+    ts(T.CORR[:], q_, 15.0, OP.is_lt, -128.0, OP.mult)
+    need("v", x0, x1)
+    c_sd = tt(T.SD[:], T.SD0[:], T.SD1[:], OP.add)
+    need("v", p_wa)
+    c_w = vcopy(T.W3[:, 0:384], T.PWA[:, 0:384])
+    need("v", p_l)
+    c_l = vcopy(T.LST[:], T.PSL[:, 0:24, :])
+    need("t", s_t1, s_w, c_w)
+    for b in range(8):
+        p_wh = mm((T.PE1 if b > 3 else T.PWA)[:, 128 * (b % 4):128 * (b % 4) + 128], T.RB[:, b, :], T.T1[:])
+
+    need("q", c_bo, c_one, s_rb)
+    for b in (5, 6, 7, 4, 0, 1, 2, 3):
+        k_dg = did("q", g.affine_select(T.DG[:, b, :], T.RB[:, b, :], [[0, 8], [0, 2], [1, 8]], OP.is_equal, 0.0, -b, 0))
+    k_rst = did("q", g.affine_select(T.RST[:], T.ONE[:, 0:64], [[0, 4], [1, 16]], OP.not_equal, 0.0, 0, 0))
+    k_io1 = iota(T.IO1[:], [[1, 64]], 0, 1)
+    k_nb = iota(T.NB[:, 8 * rank:8 * rank + 8], [[0, 8]])
+
+    src = T.W3
+    need("v", s_w3)
+    for k, dst in ((2, T.W2), (1, T.W1), (0, T.W0)):
+        need("v", c_w, c_l)
+        need("s", s_w, c_l)
+        c_w = vcopy(dst[:, 0:512], src[:, 0:512].indirect(T.LST[:, k, 0:32]))
+        s_w = scopy(dst[:, 512:1024], src[:, 512:1024].indirect(T.LST[:, k, 32:64]))
+        src = dst
+
+    def to_lists(lst, sc, win, slots, at=0):
+        for i, s in enumerate(slots):
+            x = scan(sc[:, 128 * (at + i):128 * (at + i) + 128], T.SD[:], win[:, 128 * s:128 * s + 128], OP.add, OP.max)
+        need("v", x)
+        n = len(slots)
+        return ts(lst[:, 8 * at:8 * at + 8 * n], sc[:, 128 * at + 15:128 * (at + n):16], T.CORR[:], OP.add)
+
+    def w0(b):
+        return T.W0[:, 128 * b:128 * b + 128]
+
+    def qm(b):
+        return T.QM[:, 128 * b:128 * b + 128]
+    need("v", c_w, s_w, c_sd)
+    l1 = to_lists(T.LA, T.SCA, T.W0, [4, 6], 2)
+    l0 = to_lists(T.LA, T.SCA, T.W0, [0, 2])
+    need("v", l0)
+    c_q = vcopy(qm(0), w0(1).indirect(T.LA[:, 0:8]))
+    need("s", l1)
+    s_q2 = scopy(qm(2), w0(5).indirect(T.LA[:, 16:24]))
+    s_q = scopy(qm(3), w0(7).indirect(T.LA[:, 24:32]))
+    need("s", l0)
+    s_q1 = scopy(qm(1), w0(3).indirect(T.LA[:, 8:16]))
+    need("v", c_q, s_q2)
+    c_lb = to_lists(T.LB, T.SCB, T.QM, [0, 2])
+    need("v", c_lb, s_q1)
+    c_h = vcopy(T.HM[:, 0:128], qm(1).indirect(T.LB[:, 0:8]))
+    need("s", c_lb, s_q1)
+    s_h = scopy(T.HM[:, 128:256], qm(3).indirect(T.LB[:, 8:16]))
+    need("v", c_h)
+    c_lc = to_lists(T.LC, T.SCC, T.HM, [0])
+    need("v", c_lc, s_h)
+
+    def slot_l(r):
+        return T.LL[:, 8 * r:8 * r + 8]
+    if rank + 1 < NR:
+        c_m = vcopy(T.MM[:], T.HM[:, 128:256].indirect(T.LC[:]))
+        need("v", c_m)
+        c_lm = to_lists(slot_l(rank), T.SCM, T.MM, [0])
+        need("q", c_lm)
+        send("e1", later(rank), slot_l(rank), lambda d: slot_l(rank))
+
+    s_m6 = scopy(T.M6[:], w0(6).indirect(T.LB[:, 8:16]))
+    s_r3 = scopy(T.R3[:], w0(2).indirect(T.LB[:, 0:8]))
+
+    def choose(out, what):
+        for i, (b, win) in enumerate(what):
+            x = mm(out, T.DG[:, b, :], win, i == 0, i + 1 == len(what))
+        return x
+    need("t", s_m6, c_h, k_dg, k_xr, s_w, c_lc)
+    p_z = choose(T.PWB[:, 0:128], [(4, T.XR[:]), (5, w0(4)), (6, qm(2)), (7, T.M6[:])])
+    need("v", p_wh)
+    c_wh = vcopy(T.WH[:, 0:512], T.PWA[:])
+    need("s", p_wh)
+    s_wh = scopy(T.WH[:, 512:1024], T.PE1[:])
+    need("s", p_z)
+    s_z = scopy(T.ZB[:], T.PWB[:, 0:128])
+    need("s", c_xt, c_sel, c_mg)
+    s_xs = scopy(T.XS[:], T.XT[:], scale=1.0 / 512.0)
+    for gg in range(4):
+        for u in range(2):
+            s_lh = scopy(T.LSH[:, :, :, 16 * gg + 8 * u:16 * gg + 8 * u + 8], T.SEL[:, 2 * u:2 * u + 2], scale=T.MG[:, gg:gg + 1])
+    c_xb = vcopy(T.XB[:], T.X[:])
+    need("v", s_z)
+    c_g4 = vcopy(T.G4[:], T.ZB[:].indirect(T.LC[:]))
+    need("t", s_xs, k_xr, c_one, s_lh)
+    for t in range(2):
+        mm(T.PTT[64 * t:64 * t + 64, 1, :], T.ONE[0:1, 0:64], T.XR[0:1, :], True, False)
+        p_tt = mm(T.PTT[64 * t:64 * t + 64, 1, :], T.LSH[:, 0, t, :], T.XS[:, t, :], False, True)
+    need("t", c_g4, s_r3)
+    p_pw = choose(T.PWB[:, 128:256], [(0, T.XR[:]), (1, w0(0)), (2, qm(0)), (3, T.R3[:])]
+                  + [(b, T.G4[:]) for b in (4, 5, 6, 7)])
+    need("v", dem)
+    c_em = ts(T.EMF[:], T.EM[:], -31.5, OP.add)
+    a = ts(T.EI0[:], T.EM[:], 63, OP.bitwise_and)
+    need("s", c_xb)
+    act(T.SG[:, :, 0, :], T.XB[:], ACT.Sign, bias=-127.5)
+    act(T.SG[:, :, 1, :], T.XB[:], ACT.Sign, bias=-255.5)
+    need("v", a)
+    c_eb = ts(T.EB[:, :, 0, :], T.EI0[:], 1.0 / 64.0, OP.mult)
+    need("s", c_em)
+    a = scopy(T.EA[:], T.EMF[:], scale=1.0 / 64.0, bias=12582912.0)
+    need("s", a)
+    s_eb = scopy(T.EB[:, :, 1, :], T.EA[:], scale=1.0 / 64.0, bias=-196608.0)
+    need("t", c_eb, s_eb)
+    for k in range(2):
+        for t in range(2):
+            o = T.PE0[64 * t:64 * t + 64, 256 * k:256 * k + 256]
+            mm(o, T.LSH[:, k, t, :], T.SG[:, t], True, False)
+            p_e = mm(o, T.LSH[:, k, t, :], T.EB[:, t], False, True)
+    need("v", c_wh)
+    c_hh = ts(T.HH[:, 0:512], T.WH[:, 0:512].indirect(T.LST[:, 0, 0:32]), 1.0 / 512.0, OP.mult)
+    need("s", s_wh)
+    s_hh = scopy(T.HH[:, 512:1024], T.WH[:, 512:1024].indirect(T.LST[:, 0, 32:64]), scale=1.0 / 512.0)
+    need("t", c_hh, s_hh)
+    mm(T.PTT[:, 0, :], T.ONE[0:1, :], T.XR[0:1, :], True, False)
+    for b in range(8):
+        p_ta = mm(T.PTT[:, 0, :], T.DG[:, b, :], T.HH[:, 128 * b:128 * b + 128], False, b == 7)
+    need("v", p_pw)
+    c_pw = vcopy(T.PW[:], T.PWB[:, 128:256])
+    need("v", c_kp, k_key)
+    a = ts(T.TU[:], T.KEY[:], T.KP[:], OP.is_gt)
+    c_mk = ts(T.MK[:], T.J16[:, 0:64], q_, OP.is_equal)
+    need("v", a)
+    c_tri = tt(T.TRI[:], T.TU[:], T.BO[:], OP.mult)
+
+    def fold(e, lst, win, c):
+        for i in lst:
+            need(e, arrive("e1", i))
+            o = T.FB[:, 128 * i:128 * i + 128]
+            c = (vcopy if e == "v" else scopy)(o, win.indirect(slot_l(i)))
+            need(e, c)
+            win = o
+        return win, c
+
+    def look(out, win, by, *toks):
+        need("v", *toks)
+        return vcopy(out, win.indirect(by))
+    need("v", c_pw, k_ir)
+    need("s", k_ir)
+    if rank == 0:
+        st = vcopy(T.S0[:, 0:1], T.PW[:, 0:1])
+    else:
+        by = T.LL[:, 0:1]
+        far = list(range(mine[0] - 1, 0, -1))
+        if first:
+            win, c = fold("v", list(range(rank - 1, 0, -1)), T.PW[:], c_pw)
+            a = arrive("e1", 0)
+        elif j == 0:
+            low, c = fold("s", far[-1:], T.IR[:], k_ir)
+            win, _ = fold("v", far[:-1], T.PW[:], c_pw)
+            a = look(T.X4[:], low, by, arrive("e1", 0), c)
+            by = T.X4[:, 0:1]
+        else:
+            own = list(range(rank - 1, mine[0] - 1, -1))
+            few = len(own) < len(far)
+            mid, c = fold("s", far[:-1] if few else far, T.IR[:], k_ir)
+            win, _ = fold("v", own, T.PW[:], c_pw)
+            a = arrive("e1", 0)
+            if few:
+                low, _ = fold("v", far[-1:], T.IR[:], k_ir)
+                a = look(T.X1[:], low, by, a)
+                by = T.X1[:, 0:1]
+            a = look(T.X4[:], mid, by, a, c)
+            by = T.X4[:, 0:1]
+        st = look(T.S0[:], win, by, a)
+    need("s", p_e)
+    s_ew = act(T.EW[:], T.PE0[:], ACT.Relu, scale=64.0, bias=-63.0)
+    need("v", p_tt, p_ta, k_kc, st)
+    a = ts(T.TA[:, 0, :], T.PTT[:, 0, :], T.S0[:, 0:1], OP.subtract, 512.0, OP.mult)
+    b = ts(T.S1[:], T.S0[:, 0:1], T.M1[:], OP.mult)
+    need("v", a)
+    a = did("v", V.tensor_reduce(T.RA[:], T.TA[:, 0, :], AX.X, OP.min, apply_absolute_value=True))
+    need("v", a, b)
+    st = ts(T.ST[:, 0:1], T.RA[:], T.MU[:], OP.mult, T.S1[:], OP.add)
+    need("v", st)
+    a = ts(T.TA[:, 1, :], T.PTT[:, 1, :], T.ST[:, 0:1], OP.subtract, 512.0, OP.mult)
+    ts(T.OFP[:, 0:2], T.KC[:, 0:2], T.ST[:, 0:1], OP.add)
+    need("v", a)
+    st = did("v", V.tensor_reduce(T.ST[:, 1:2], T.TA[:, 1, :], AX.X, OP.min, apply_absolute_value=True))
+    need("v", st)
+    c_of = ts(T.OFP[:, 2:4], T.KC[:, 2:4], T.ST[:, 1:2], OP.add)
+    need("v", c_of, s_ew, c_mk)
+    c_gv = tt(T.GV[:], T.EW[:].indirect(T.OFP[:]), T.MK[:], OP.mult)
+    need("v", c_gv)
+    a = ts(T.FL[:], T.GV[:], 0.0, OP.is_gt)
+    need("v", a)
+    c_inc = scan(T.INC[:], T.ONE[:, 0:64], T.FL[:], OP.mult, OP.add)
+    need("t", c_inc, c_tri, s_w3, c_wh)
+    p_b = mm(T.PSO[:, 0:1], T.TRI[:], T.INC[:, 63:64])
+    p_n = mm(T.PWA[:, 0:1], T.BO[:], T.INC[:, 63:64])
+    need("v", k_rst)
+    c_scn = scan(T.SCN[:], T.RST[:], T.GV[:], OP.mult, OP.add)
+    need("v", p_b, c_inc)
+    c_pos = ts(T.POS[:], T.INC[:, 15:64:16], T.PSO[:, 0:1], OP.add)
+    need("s", p_n, k_nb)
+    s_n = scopy(T.NB[:, 8 * rank:8 * rank + 1], T.PWA[:, 0:1])
+    if rank + 1 < NR:
+        need("q", s_n)
+        send("en", later(rank), T.NB[:, 8 * rank:8 * rank + 8], lambda d: T.NB[:, 8 * rank:8 * rank + 8])
+    need("s", c_scn)
+    s_nv = scopy(T.NV[:], T.SCN[:, 15:64:16], scale=-1.0)
+    need("s", c_pos, k_io1)
+    a = act(T.OD[:], T.IO1[:], ACT.Abs, scale=-1.0, bias=T.POS[:, 3:4])
+    need("s", a, s_nv)
+    s_oh = act(T.OH[:, 3, :], T.OD[:], ACT.Relu, scale=T.NV[:, 3:4], bias=T.SCN[:, 63:64])
+    s_own = scopy(T.OWN[:], T.PWA[:, 0:1])
+    need("v", c_pos, c_scn, k_io1)
+    for i in range(4):
+        if i < 3:
+            a = ts(T.OH[:, i, :], T.IO1[:], T.POS[:, i:i + 1], OP.is_equal, T.SCN[:, 16 * i + 15:16 * i + 16], OP.mult)
+        need("t", a if i < 3 else s_oh)
+        p_a = mm(T.PSA[:, 256:320], T.BO[:], T.OH[:, i, :], i == 0, i == 3)
+    a = c_qi = ts(T.QI[:], T.IR[:, 0:17:16], q_, OP.add, float(32 * rank), OP.add)
+    need("v", p_a)
+    c_a = ts(T.F[:, 64:128], T.PSA[:, 256:320], -1.0, OP.add)
+    need("q", c_a)
+    n = 64 if rank + 1 < NR else 16
+    send("ev", beside(rank), T.F[:, 64:64 + n], lambda d: T.F[:, 0:n] if d > rank else T.F[:, 128:128 + n])
+
+    lo = 0 if rank > 0 else 64
+    hi = 192 if rank + 2 < NR else 144 if rank + 1 < NR else 128
+    u = T.QI[:]
+    need("v", s_own)
+    c_b1 = ts(T.B1[:], T.OWN[:], -1.0, OP.mult, 64.0, OP.add)
+    if rank > 0:
+        for i in range(rank):
+            need("v", arrive("en", i))
+        b = did("v", V.tensor_reduce(T.BEG[:], T.NB[:, 0:8 * rank - 7:8], AX.X, OP.add))
+        c_a1 = ts(T.A1[:], T.NB[:, 8 * rank - 8:8 * rank - 7], 64.0, OP.subtract)
+        need("v", b, c_qi)
+        u = T.U[:]
+        a = ts(u, T.QI[:], T.BEG[:], OP.subtract)
+    need("v", a)
+    o = u
+    if rank + 1 < NR:
+        need("v", c_b1)
+        b = ts(T.U1[:], u, T.OWN[:], OP.is_ge, T.B1[:], OP.mult)
+    if rank > 0:
+        need("v", c_a1)
+        c = ts(T.U3[:], u, 0.0, OP.is_lt, T.A1[:], OP.mult)
+    if rank + 1 < NR:
+        need("v", b)
+        o = T.U2[:]
+        a = tt(o, u, T.U1[:], OP.add)
+    if rank > 0:
+        need("v", a, c)
+        a = tt(T.U4[:], o, T.U3[:], OP.add)
+        o = T.U4[:]
+    need("v", a)
+    a = ts(T.OF2[:], o, float(64 - lo), OP.add)
+    for i in beside(rank):
+        need("v", arrive("ev", i))
+    need("v", a, c_a)
+    a = vcopy(T.Y1[:], T.F[:, lo:hi].indirect(T.OF2[:]))
+    need("y", a)
+    g.sync.dma_start(T.y[:, :], T.Y1[0:128:16, :]).then_inc(T.sem.dy, 16)
+    need("y", ("dy", 16))
+    for e in ("v", "s", "t", "q"):
+        need("q", (e, cnt[e]))
+    need("q", ("ls", sent[0]))

@@ -2,23 +2,21 @@ from concourse.bass import DstId, RemoteDMATransfer
 from concourse.mybir import dt, AluOpType, AxisListType, ActivationFunctionType
 
 _BUF = {
-    "int32": "PI:1 CI:4 SYI:2x32 X:2x128 XA:2x128 EM:2x128 EI0:2x128",
-    "uint16": "LST:3x64 LA:32 LB:16 LC:8 LL:64 X1:16 X4:16 OFP:4 OF2:2",
-    "float32": "PF:1 CF:4 RI:128 IR:128 GC:128 J16:128 KEY:128 MG:4 MS:16 S0:16 Q1:1 CORR:1 MU:1 M1:1 K1:1 KP:1 RA:1 S1:1 "
-               "SD0:128 SD1:128 KC:4 EMF:2x128 EA:2x128 QI:2 ST:2 TA:2x128 NV:4 OWN:1 BEG:1 A1:1 B1:1 U:2 U1:2 U2:2 U3:2 "
-               "U4:2 Y1:32",
-    "bfloat16": "R:128 XR:128 BRR:192 DG:8x128 ZB:128 G4:128 R3:128 BO:128 RB:8x128 ONE:128 IO1:64 TU:128 TRI:128 "
-                "SYB:2x32 XT:2x128 XS:2x128 XB:2x128 EB:2x2x128 SG:2x2x128 SEL:4x2x8 LS:4x2x64 LSH:2x2x64 YB:16x64 T3:128 "
-                "T1:128 WH:1024 HH:1024 W3:1024 W2:1024 W1:1024 W0:1024 QM:512 HM:256 MM:128 SD:128 SCA:512 SCB:256 "
-                "SCC:128 SCM:128 FB:896 M6:128 PW:128 EW:512 MK:64 RST:64 GV:64 SCN:64 FL:64 INC:64 POS:4 OH:4x64 OD:64 "
-                "NB:64 F:192",
+    "int32": "PI:1 CI:5 SYH:16 SYN:2 X:2x128 XA:2x128 EM:2x128 EI0:2x128",
+    "uint16": "OFS:16 LST:256 LA:32 LB:16 LC:8 LL:64 X1:16 X4:16 OFP:4 OF2:2",
+    "float32": "CF:5 MS:4 CORR:1 SYF:2 MU:1 M1:1 LO:1 HI:1 KC:4 KB:2 S0:16 S1:1 RA:3 TA:3x128 OWN:1 BEG:1 A1:1 B1:1 "
+               "QI:2 QO:2 QL:2 U:2 U1:2 U3:2 Y1:32 SCN:64",
+    "bfloat16": "ONE:130 IW:256 ID:128 IS:128 R:128 J16:144 SD0:144 SD:128 DG:4x128 X512:128 MK:64 MKI:64 BO1:128 BO:128 "
+                "TRI:128 RST:64 SYB:16 XI:8x2x16 TL:256 UP:128 LSB:256 ST:64 SEL:2x2x16 LS:2x2x130 W3:4x256 W2:4x256 W1:4x256 "
+                "W0:2x2x256 SCA:512 SCB:256 SCC:128 SCM:128 QM:4x128 HM:256 MM:128 RM:256 ZL:128 ZH:128 PW:128 FB:896 "
+                "XB:2x128 SG:2x2x128 EB:2x2x128 EW:512 GV:64 FL:68 INC:68 OH:4x64 NB:64 F:192",
 }
 SCRATCH = {n: ("sbuf", [128] + [int(x) for x in d.split("x")], t)
            for t, l in _BUF.items() for n, d in (w.split(":") for w in l.split())}
-for _n, _d in (("PSA", [512]), ("PSL", [64, 8]), ("PWA", [512]), ("PWB", [512]), ("PTT", [4, 128]), ("PE0", [512]),
-               ("PE1", [512]), ("PSO", [512])):
+for _n, _d in (("PSA", [512]), ("PSD", [512]), ("PZ", [512]), ("PT", [4, 128]), ("PE0", [512]), ("PSO", [512]),
+               ("PN", [512])):
     SCRATCH[_n] = ("psum", [128] + _d, "float32")
-SEMAPHORES = (["v", "s", "t", "q", "dsy", "dx", "dxs", "dem", "dy", "ls"]
+SEMAPHORES = (["v", "s", "t", "q", "dsh", "dsn", "dx0", "dx1", "dem", "dy", "ls"]
               + [p + "_%d" % j for p in ("e1", "en", "ev") for j in range(8)])
 
 
@@ -61,8 +59,11 @@ def rank_program(g, core, T, topo):
     def fill(ap, x):
         return did("v", V.memset(ap, x))
 
-    def scan(out, d0, d1, o0, o1):
-        return did("v", V.tensor_tensor_scan(out, d0, d1, 0.0, o0, o1))
+    def scan(out, d0, d1, o0, o1, init=0.0):
+        return did("v", V.tensor_tensor_scan(out, d0, d1, init, o0, o1))
+
+    def reduce_(out, in_, op, **k):
+        return did("v", V.tensor_reduce(out, in_, AX.X, op, **k))
 
     def act(out, in_, func, **k):
         return did("s", S.activation(out, in_, func, **k))
@@ -75,6 +76,9 @@ def rank_program(g, core, T, topo):
 
     def iota(out, pattern, cm=0, base=0):
         return did("q", g.iota(out, pattern, base, cm, allow_small_or_imprecise_dtypes=True))
+
+    def where(out, in_, pattern, op, base, cm):
+        return did("q", g.affine_select(out, in_, pattern, op, 0.0, base, cm))
 
     def same(r, r2):
         return topo.chip(T.cores[r]) == topo.chip(T.cores[r2])
@@ -103,248 +107,225 @@ def rank_program(g, core, T, topo):
         return ("%s_%d" % (kind, r), [len(es) for ds, es in plan(r, dsts) if rank in ds][0])
     sent = [0]
 
-    def send(kind, dsts, src_, where):
+    def send(kind, dsts, src_, at):
         trs = []
         for ds, es in plan(rank, dsts):
             adr = [topo.addr(T.cores[d]) for d in ds]
             trs.append(RemoteDMATransfer(dst_ids=[DstId(rid=x[0], pnc=x[1]) for x in adr],
                                          dma_engine_mask=sum(1 << e for e in es),
-                                         remote_sem=T.sem["%s_%d" % (kind, rank)], srcs=[src_], dsts=[where(d) for d in ds]))
+                                         remote_sem=T.sem["%s_%d" % (kind, rank)], srcs=[src_], dsts=[at(d) for d in ds]))
             sent[0] += len(es)
         g.remote_dma_fused(trs, local_sem=T.sem.ls)
 
-    g.sync.dma_start(T.X[:, 0, :], T.nx[0:4, :]).then_inc(T.sem.dx, 16)
-    S.dma_start(T.X[:, 1, :], T.nx[4:8, :]).then_inc(T.sem.dxs, 16)
-    g.sync.dma_start(T.SYI[0:4, 0, :], T.sy[0:4, :]).then_inc(T.sem.dsy, 16)
-    S.dma_start(T.SYI[0:4, 1, :], T.sy[4:8, :]).then_inc(T.sem.dsy, 16)
-    g.sync.dma_start(T.EM[:, 0, :], T.em[0:4, :]).then_inc(T.sem.dem, 16)
-    g.sync.dma_start(T.EM[:, 1, :], T.em[4:8, :]).then_inc(T.sem.dem, 16)
-    dsy, dx, dxs, dem = ("dsy", 32), ("dx", 16), ("dxs", 16), ("dem", 32)
+    g.sync.dma_start(T.X[:, 0, :], T.nx[0:8:2, :]).then_inc(T.sem.dx0, 16)
+    S.dma_start(T.SYH[0:16, :], T.sy[:, :]).then_inc(T.sem.dsh, 16)
+    S.dma_start(T.X[:, 1, :], T.nx[1:8:2, :]).then_inc(T.sem.dx1, 16)
+    g.sync.dma_start(T.SYN[:], T.sy[:, :]).then_inc(T.sem.dsn, 16)
+    g.sync.dma_start(T.EM[:, 0, :], T.em[0:8:2, :]).then_inc(T.sem.dem, 16)
+    g.sync.dma_start(T.EM[:, 1, :], T.em[1:8:2, :]).then_inc(T.sem.dem, 16)
+    dsh, dsn, dx, dem = ("dsh", 16), ("dsn", 16), [("dx0", 16), ("dx1", 16)], ("dem", 32)
 
-    k_pi = did("q", g.iota(T.PI[:], [[0, 1]], 0, 1))
-    k_gc = iota(T.GC[:], [[1, 8], [0, 16]])
-    k_ir = iota(T.IR[:], [[1, 128]])
-    k_ri = iota(T.RI[0:4, :], [[1, 4], [0, 32]])
-    k_pf = iota(T.PF[:], [[0, 1]], 1)
-    k_j16 = iota(T.J16[:], [[0, 8], [1, 16]])
-    k_br = iota(T.BRR[0:1, :], [[0, 6], [128, 4], [0, 8]])
-    k_xr = iota(T.XR[:], [[1, 128]])
-    k_key = iota(T.KEY[:], [[0, 8], [1, 2], [2, 8]])
-    k_kc = iota(T.KC[:], [[128, 4]])
-
-    c_ls0 = fill(T.LS[:], 0.0)
-    need("v", k_pi)
-    for i, (x, op) in enumerate(((15, OP.bitwise_and), (31, OP.bitwise_and), (5, OP.arith_shift_right),
-                                 (4, OP.arith_shift_right))):
-        a = ts(T.CI[:, i:i + 1], T.PI[:], x, op)
-    need("v", a)
-    c_cf = vcopy(T.CF[:], T.CI[:])
-    q_, a_, gt_, gp_ = [T.CF[:, i:i + 1] for i in range(4)]
-    need("v", c_cf, k_gc)
-    c_bo = ts(T.BO[:], T.GC[:], gp_, OP.is_equal)
-    c_mu = ts(T.MU[:], q_, 8.0, OP.is_ge)
-    ts(T.M1[:], q_, 8.0, OP.is_lt)
-    need("v", k_ir)
-    c_ms = ts(T.MS[:], T.IR[:, 0:16], q_, OP.is_equal)
-    c_mg = ts(T.MG[:], T.IR[:, 0:4], gt_, OP.is_equal)
     c_one = fill(T.ONE[:], 1.0)
-    need("v", c_mu)
-    c_k1 = ts(T.K1[:], T.MU[:], -15.0, OP.mult)
-    need("s", c_bo, c_ms)
-    for b in range(8):
-        s_rb = scopy(T.RB[:, b, :], T.BO[:], scale=T.MS[:, b:b + 1])
-    need("v", c_k1)
-    c_kp = ts(T.KP[:], q_, 2.0, OP.mult, T.K1[:], OP.add)
-    need("v", k_ri, k_pf)
-    c_r = ts(T.R[0:4, :], T.RI[0:4, :], T.PF[0:4, :], OP.is_equal)
-    need("v", dsy)
-    c_syb = vcopy(T.SYB[0:4], T.SYI[0:4])
-    need("t", c_syb, c_r)
-    for k in range(4):
-        p_rep = mm(T.PSA[:, 16 * k:16 * k + 16], T.R[0:4, :], T.SYB[0:4, :, k:32:4])
-    need("v", dx, dxs)
-    a = ts(T.XA[:], T.X[:], 127, OP.bitwise_and)
-    need("v", p_rep)
-    c_sel = ts(T.SEL[:], T.PSA[:, 0:64], a_, OP.is_equal)
-    need("v", a)
-    c_xt = vcopy(T.XT[:], T.XA[:])
-    need("s", c_sel, c_mg, c_ls0)
-    for gg in range(4):
-        s_ls = scopy(T.LS[:, :, :, 16 * gg:16 * gg + 8], T.SEL[:], scale=T.MG[:, gg:gg + 1])
-    need("t", s_ls, c_xt)
-    for t in range(2):
-        p_t3 = mm(T.PSA[64 * t:64 * t + 64, 128:256], T.LS[:, 3, t, :], T.XT[:, t, :])
-    need("s", p_t3)
-    s_t3 = scopy(T.T3[:], T.PSA[:, 128:256])
-    need("v", c_xt, c_mg)
-    c_yb = []
-    for t in range(2):
-        for gg in range(4):
-            a = ts(T.YB[:, 8 * t:8 * t + 8, 16 * gg:16 * gg + 16], T.XT[:, t, :], T.MG[:, gg:gg + 1], OP.mult)
-        c_yb.append(a)
+    k_pi = did("q", g.iota(T.PI[:], [[0, 1]], 0, 32))
+    need("q", c_one)
+    k_r = where(T.R[0:16, :], T.ONE[0:16, 0:128], [[1, 16], [0, 8]], OP.is_equal, 0, -1)
+    k_j16 = iota(T.J16[:], [[0, 9], [1, 16]])
+    k_up = iota(T.UP[:], [[0, 8], [128, 2], [0, 8]])
+    k_id = where(T.ID[:], T.ONE[:, 0:128], [[-1, 128]], OP.is_equal, 0, 1)
+    k_bo1 = where(T.BO1[:], T.ONE[:, 0:128], [[-16, 8], [0, 16]], OP.is_ge, 0, 1)
+    k_rst = where(T.RST[:], T.ONE[:, 0:64], [[0, 4], [1, 16]], OP.not_equal, 0, 0)
+    need("q", k_bo1)
+    k_bo = where(T.BO[:], T.BO1[:], [[16, 8], [0, 16]], OP.is_ge, 15, -1)
 
-    def lists(t):
-        need("t", c_one, k_br)
-        mm(T.PSL[64 * t:64 * t + 64, 0:24, :], T.ONE[0:1, 0:64], T.BRR[0:1, :], True, False)
-        need("t", c_yb[t], c_sel)
-        for c in range(8):
-            x = mm(T.PSL[64 * t:64 * t + 64, 0:24, c], T.YB[:, 8 * t + c, :], T.SEL[:, 0:3, t, :], False, c == 7)
-        return x
-    lists(0)
-    need("t", s_t3, s_rb)
-    for b in range(4):
-        p_wb = mm(T.PWB[:, 128 * b:128 * b + 128], T.RB[:, 4 + b, :], T.T3[:])
-    for b in range(3):
-        p_wa = mm(T.PWA[:, 128 * b:128 * b + 128], T.RB[:, b, :], T.T3[:])
-    p_w3 = mm(T.PSO[:, 0:128], T.RB[:, 3, :], T.T3[:])
-    p_l = lists(1)
-    for t in range(2):
-        p_t1 = mm(T.PSA[64 * t:64 * t + 64, 320:448], T.LS[:, 1, t, :], T.XT[:, t, :])
-    need("s", p_wb)
-    s_w = scopy(T.W3[:, 512:1024], T.PWB[:])
-    need("s", p_w3)
-    s_w3 = scopy(T.W3[:, 384:512], T.PSO[:, 0:128])
-    need("s", p_t1)
-    s_t1 = scopy(T.T1[:], T.PSA[:, 320:448])
-    need("v", k_j16)
-    a = ts(T.Q1[:], q_, 1.0, OP.add)
-    x0 = ts(T.SD0[:], T.J16[:], q_, OP.is_equal, -65536.0, OP.mult)
+    need("v", c_one)
+    c_xr = scan(T.IW[:, 0:128], T.ONE[:, 0:128], T.ONE[:, 0:128], OP.mult, OP.add, -1.0)
+    need("v", k_pi)
+    for i, (sh, m) in enumerate(((5, 15), (0, 255), (6, 3), (5, 1))):
+        a = ts(T.CI[:, i:i + 1], T.PI[:], sh, OP.arith_shift_right, m, OP.bitwise_and)
     need("v", a)
-    x1 = ts(T.SD1[:], T.J16[:], T.Q1[:], OP.is_equal, 128.0, OP.mult)
+    c_cf = vcopy(T.CF[:, 0:4], T.CI[:, 0:4])
+    q_, c32, b4, mu = [T.CF[:, i:i + 1] for i in range(4)]
+    c_fl = fill(T.FL[:, 64:68], 0.0)
+    need("v", c_cf, c_xr)
+    c_ms = ts(T.MS[:], T.IW[:, 0:4], b4, OP.is_equal)
     ts(T.CORR[:], q_, 15.0, OP.is_lt, -128.0, OP.mult)
-    need("v", x0, x1)
-    c_sd = tt(T.SD[:], T.SD0[:], T.SD1[:], OP.add)
-    need("v", p_wa)
-    c_w = vcopy(T.W3[:, 0:384], T.PWA[:, 0:384])
-    need("v", p_l)
-    c_l = vcopy(T.LST[:], T.PSL[:, 0:24, :])
-    need("t", s_t1, s_w, c_w)
-    for b in range(8):
-        p_wh = mm((T.PE1 if b > 3 else T.PWA)[:, 128 * (b % 4):128 * (b % 4) + 128], T.RB[:, b, :], T.T1[:])
+    ts(T.LO[:], q_, 8.0, OP.is_lt, 512.0, OP.mult)
+    ts(T.HI[:], q_, 8.0, OP.is_ge, 512.0, OP.mult)
+    ts(T.MU[:], mu, 512.0, OP.mult)
+    ts(T.M1[:], mu, 1.0, OP.is_lt)
+    need("v", k_j16)
+    c_sd0 = ts(T.SD0[:], T.J16[:], q_, OP.is_equal, -65536.0, OP.mult)
 
-    need("q", c_bo, c_one, s_rb)
-    for b in (5, 6, 7, 4, 0, 1, 2, 3):
-        k_dg = did("q", g.affine_select(T.DG[:, b, :], T.RB[:, b, :], [[0, 8], [0, 2], [1, 8]], OP.is_equal, 0.0, -b, 0))
-    k_rst = did("q", g.affine_select(T.RST[:], T.ONE[:, 0:64], [[0, 4], [1, 16]], OP.not_equal, 0.0, 0, 0))
-    k_io1 = iota(T.IO1[:], [[1, 64]], 0, 1)
+    need("s", c_one, c_xr)
+    for u in range(2):
+        for h in range(2):
+            s_z = scopy(T.LS[:, u, h, :], T.ONE[:], scale=0.0)
+    s_iw = scopy(T.IW[:, 128:256], T.IW[:, 0:128])
+    s_x5 = scopy(T.X512[0:1, :], T.IW[0:1, 0:128], scale=512.0)
+    need("s", k_id, c_ms)
+    s_is = scopy(T.IS[:], T.ID[:], scale=-1.0 / 512.0)
+    for m in range(4):
+        s_dg = scopy(T.DG[:, m, :], T.ID[:], scale=T.MS[:, m:m + 1])
+
+    c_a = []
+    for h in range(2):
+        need("v", dx[h])
+        c_a.append(ts(T.XA[:, h, :], T.X[:, h, :], 127, OP.bitwise_and))
+        if h == 0:
+            need("v", dsh)
+            c_syb = vcopy(T.SYB[0:16, :], T.SYH[0:16, :])
+            need("t", c_syb, k_r)
+            p_of = mm(T.PSA[:, 0:16], T.R[0:16, :], T.SYB[0:16, :])
+    for h in range(2):
+        need("v", c_a[h])
+        c_xi = vcopy(T.XI[:, :, h, :], T.XA[:, h, :])
+    need("v", dsn)
+    c_syf = vcopy(T.SYF[:], T.SYN[:])
+    need("v", p_of)
+    c_ofs = ts(T.OFS[:], T.PSA[:, 0:16], c32, OP.add)
+    need("v", c_xi)
+    c_tl = did("v", V.transpose(T.TL[:], T.XI[:]))
+    need("v", c_syf)
+    for u in range(2):
+        c_st = ts(T.ST[:, 32 * u:32 * u + 32], T.IW[:, 0:32], T.SYF[:, u:u + 1], OP.is_equal)
+    need("v", c_tl, c_ofs, k_up)
+    c_l = [tt(T.LSB[:, 128 * e:128 * e + 128], T.TL[:].indirect(T.OFS[:, 8 * e:8 * e + 8]), T.UP[:], OP.add)
+           for e in range(2)]
+    for e in range(2):
+        need("v", c_l[e])
+        c_l[e] = vcopy(T.LST[:, 128 * e:128 * e + 128], T.LSB[:, 128 * e:128 * e + 128])
+        if e == 0:
+            need("v", c_st)
+            c_sel = did("v", V.transpose(T.SEL[:], T.ST[:]))
+
+    need("q", c_sel, s_z)
+    for a in range(4):
+        need("q", ("q", cnt["q"]))
+        for h in range(2):
+            o = 2 + 32 * a + 16 * h
+            k_ls = where(T.LS[32 * a:32 * a + 32, :, h, o:o + 16], T.SEL[32 * a:32 * a + 32, :, h, :], [[0, 32]],
+                         OP.is_equal, 0, 0)
+    need("q", k_ls)
+    iota(T.KC[:, 0:2], [[1, 2]])
+    iota(T.KC[:, 2:4], [[128, 2]], 0, 256)
     k_nb = iota(T.NB[:, 8 * rank:8 * rank + 8], [[0, 8]])
+    need("q", k_bo)
+    k_tri = where(T.TRI[:], T.BO[:], [[1, 128]], OP.is_gt, 0, -1)
+    need("t", c_sd0, k_id, s_is)
+    mm(T.PSD[:, 0:128], T.ID[:], T.SD0[:, 16:144], True, False)
+    p_sd = mm(T.PSD[:, 0:128], T.IS[:], T.SD0[:, 15:143], False, True)
+    need("s", p_sd)
+    s_sd = scopy(T.SD[:], T.PSD[:, 0:128])
+    scopy(T.MK[:], T.SD0[:, 0:64], scale=-1.0 / 65536.0)
+    s_mk = scopy(T.MKI[:], T.SD0[:, 0:64], scale=1.0 / 64.0, bias=1024.0)
+    need("t", k_ls, s_x5, c_xi)
+    for i, (u, o) in enumerate(((0, 1), (1, 1), (0, 2))):
+        mm(T.PT[:, i, :], T.ONE[0:1, 0:128], T.X512[0:1, :], True, False)
+        for h in range(2):
+            p_t = mm(T.PT[:, i, :], T.LS[:, u, h, o:o + 128], T.XI[:, :, h, :], False, h == 1)
 
-    src = T.W3
-    need("v", s_w3)
-    for k, dst in ((2, T.W2), (1, T.W1), (0, T.W0)):
-        need("v", c_w, c_l)
-        need("s", s_w, c_l)
-        c_w = vcopy(dst[:, 0:512], src[:, 0:512].indirect(T.LST[:, k, 0:32]))
-        s_w = scopy(dst[:, 512:1024], src[:, 512:1024].indirect(T.LST[:, k, 32:64]))
-        src = dst
-
-    def to_lists(lst, sc, win, slots, at=0):
-        for i, s in enumerate(slots):
-            x = scan(sc[:, 128 * (at + i):128 * (at + i) + 128], T.SD[:], win[:, 128 * s:128 * s + 128], OP.add, OP.max)
-        need("v", x)
-        n = len(slots)
-        return ts(lst[:, 8 * at:8 * at + 8 * n], sc[:, 128 * at + 15:128 * (at + n):16], T.CORR[:], OP.add)
+    def lst(e, side, k):
+        o = 128 * e + 64 * side + 16 * k
+        return T.LST[:, o:o + 16]
 
     def w0(b):
-        return T.W0[:, 128 * b:128 * b + 128]
+        return T.W0[:, b % 4 // 2, b % 2, 128 * (b // 4):128 * (b // 4) + 128]
+    tok = {}
+    need("v", c_l[0], s_iw)
+    need("s", c_l[1], s_iw)
+    for k in (3, 2, 1, 0):
+        for side in range(2):
+            for e, (qu, f) in enumerate((("v", vcopy), ("s", scopy))):
+                win = T.IW[:] if k == 3 else T["W%d" % (k + 1)][:, 2 * e + side, :]
+                out = T.W0[:, e, side, :] if k == 0 else T["W%d" % k][:, 2 * e + side, :]
+                if k < 3:
+                    need(qu, tok[e, side])
+                tok[e, side] = f(out, win.indirect(lst(e, side, k)))
+
+    def diag(sc, at, win):
+        return scan(sc[:, 128 * at:128 * at + 128], T.SD[:], win, OP.add, OP.max)
+
+    def pick(out, sc, at, n=1):
+        return ts(out, sc[:, 128 * at + 15:128 * (at + n):16], T.CORR[:], OP.add)
 
     def qm(b):
-        return T.QM[:, 128 * b:128 * b + 128]
-    need("v", c_w, s_w, c_sd)
-    l1 = to_lists(T.LA, T.SCA, T.W0, [4, 6], 2)
-    l0 = to_lists(T.LA, T.SCA, T.W0, [0, 2])
-    need("v", l0)
-    c_q = vcopy(qm(0), w0(1).indirect(T.LA[:, 0:8]))
-    need("s", l1)
-    s_q2 = scopy(qm(2), w0(5).indirect(T.LA[:, 16:24]))
-    s_q = scopy(qm(3), w0(7).indirect(T.LA[:, 24:32]))
-    need("s", l0)
-    s_q1 = scopy(qm(1), w0(3).indirect(T.LA[:, 8:16]))
-    need("v", c_q, s_q2)
-    c_lb = to_lists(T.LB, T.SCB, T.QM, [0, 2])
-    need("v", c_lb, s_q1)
+        return T.QM[:, b, :]
+    d = []
+    for i, b in enumerate((0, 4, 2, 6)):
+        need("v", tok[i // 2, 0], s_sd)
+        d.append(diag(T.SCA, i, w0(b)))
+    need("v", d[1])
+    l0 = pick(T.LA[:, 0:16], T.SCA, 0, 2)
+    need("v", d[3])
+    l1 = pick(T.LA[:, 16:32], T.SCA, 2, 2)
+    need("v", l0, tok[0, 1])
+    c_q0 = vcopy(qm(0), w0(1).indirect(T.LA[:, 0:8]))
+    c_q2 = vcopy(qm(2), w0(5).indirect(T.LA[:, 8:16]))
+    need("s", l1, tok[1, 1])
+    s_q1 = scopy(qm(1), w0(3).indirect(T.LA[:, 16:24]))
+    s_q3 = scopy(qm(3), w0(7).indirect(T.LA[:, 24:32]))
+    need("v", c_q0)
+    a = diag(T.SCB, 0, qm(0))
+    c_qi = ts(T.QI[:], T.IW[:, 0:17:16], q_, OP.add, float(32 * rank), OP.add)
+    need("v", c_q2)
+    b = diag(T.SCB, 1, qm(2))
+    need("v", a)
+    c_b0 = pick(T.LB[:, 0:8], T.SCB, 0)
+    need("v", b)
+    c_b1 = pick(T.LB[:, 8:16], T.SCB, 1)
+    need("v", c_b0, s_q1)
     c_h = vcopy(T.HM[:, 0:128], qm(1).indirect(T.LB[:, 0:8]))
-    need("s", c_lb, s_q1)
+    need("s", c_b1, s_q3)
     s_h = scopy(T.HM[:, 128:256], qm(3).indirect(T.LB[:, 8:16]))
     need("v", c_h)
-    c_lc = to_lists(T.LC, T.SCC, T.HM, [0])
-    need("v", c_lc, s_h)
+    a = diag(T.SCC, 0, T.HM[:, 0:128])
+    need("v", a)
+    c_lc = pick(T.LC[:], T.SCC, 0)
 
     def slot_l(r):
         return T.LL[:, 8 * r:8 * r + 8]
     if rank + 1 < NR:
+        need("v", c_lc, s_h)
         c_m = vcopy(T.MM[:], T.HM[:, 128:256].indirect(T.LC[:]))
         need("v", c_m)
-        c_lm = to_lists(slot_l(rank), T.SCM, T.MM, [0])
+        a = diag(T.SCM, 0, T.MM[:])
+        need("v", a)
+        c_lm = pick(slot_l(rank), T.SCM, 0)
         need("q", c_lm)
         send("e1", later(rank), slot_l(rank), lambda d: slot_l(rank))
 
-    s_m6 = scopy(T.M6[:], w0(6).indirect(T.LB[:, 8:16]))
-    s_r3 = scopy(T.R3[:], w0(2).indirect(T.LB[:, 0:8]))
-
-    def choose(out, what):
-        for i, (b, win) in enumerate(what):
-            x = mm(out, T.DG[:, b, :], win, i == 0, i + 1 == len(what))
-        return x
-    need("t", s_m6, c_h, k_dg, k_xr, s_w, c_lc)
-    p_z = choose(T.PWB[:, 0:128], [(4, T.XR[:]), (5, w0(4)), (6, qm(2)), (7, T.M6[:])])
-    need("v", p_wh)
-    c_wh = vcopy(T.WH[:, 0:512], T.PWA[:])
-    need("s", p_wh)
-    s_wh = scopy(T.WH[:, 512:1024], T.PE1[:])
+    scopy(T.RM[:, 0:128], w0(2).indirect(T.LB[:, 0:8]))
+    s_rm = scopy(T.RM[:, 128:256], w0(6).indirect(T.LB[:, 8:16]))
+    need("t", s_dg, s_iw, c_q2)
+    for m, win in enumerate((T.IW[:], T.W0[:, 0, 0, :], T.QM[:, 0:4:2, :], T.RM[:])):
+        if m == 3:
+            need("t", s_rm)
+        p_z = mm(T.PZ[:, 0:256], T.DG[:, m, :], win, m == 0, m == 3)
     need("s", p_z)
-    s_z = scopy(T.ZB[:], T.PWB[:, 0:128])
-    need("s", c_xt, c_sel, c_mg)
-    s_xs = scopy(T.XS[:], T.XT[:], scale=1.0 / 512.0)
-    for gg in range(4):
-        for u in range(2):
-            s_lh = scopy(T.LSH[:, :, :, 16 * gg + 8 * u:16 * gg + 8 * u + 8], T.SEL[:, 2 * u:2 * u + 2], scale=T.MG[:, gg:gg + 1])
+    scopy(T.ZH[:], T.PZ[:, 128:256], scale=T.HI[:])
+    s_zl = scopy(T.ZL[:], T.PZ[:, 0:128], scale=T.LO[:])
     c_xb = vcopy(T.XB[:], T.X[:])
-    need("v", s_z)
-    c_g4 = vcopy(T.G4[:], T.ZB[:].indirect(T.LC[:]))
-    need("t", s_xs, k_xr, c_one, s_lh)
-    for t in range(2):
-        mm(T.PTT[64 * t:64 * t + 64, 1, :], T.ONE[0:1, 0:64], T.XR[0:1, :], True, False)
-        p_tt = mm(T.PTT[64 * t:64 * t + 64, 1, :], T.LSH[:, 0, t, :], T.XS[:, t, :], False, True)
-    need("t", c_g4, s_r3)
-    p_pw = choose(T.PWB[:, 128:256], [(0, T.XR[:]), (1, w0(0)), (2, qm(0)), (3, T.R3[:])]
-                  + [(b, T.G4[:]) for b in (4, 5, 6, 7)])
     need("v", dem)
-    c_em = ts(T.EMF[:], T.EM[:], -31.5, OP.add)
     a = ts(T.EI0[:], T.EM[:], 63, OP.bitwise_and)
+    ts(T.EB[:, :, 1, :], T.EM[:], 1.0 / 4096.0, OP.mult, (160.0 - 31.5 / 64.0) / 64.0, OP.add)
+    need("v", a)
+    c_eb = ts(T.EB[:, :, 0, :], T.EI0[:], 1.0 / 64.0, OP.mult, 2.5, OP.add)
+    need("v", s_zl, c_lc)
+    c_pw = tt(T.PW[:], T.ZH[:].indirect(T.LC[:]), T.ZL[:], OP.add)
     need("s", c_xb)
     act(T.SG[:, :, 0, :], T.XB[:], ACT.Sign, bias=-127.5)
-    act(T.SG[:, :, 1, :], T.XB[:], ACT.Sign, bias=-255.5)
-    need("v", a)
-    c_eb = ts(T.EB[:, :, 0, :], T.EI0[:], 1.0 / 64.0, OP.mult)
-    need("s", c_em)
-    a = scopy(T.EA[:], T.EMF[:], scale=1.0 / 64.0, bias=12582912.0)
-    need("s", a)
-    s_eb = scopy(T.EB[:, :, 1, :], T.EA[:], scale=1.0 / 64.0, bias=-196608.0)
-    need("t", c_eb, s_eb)
-    for k in range(2):
-        for t in range(2):
-            o = T.PE0[64 * t:64 * t + 64, 256 * k:256 * k + 256]
-            mm(o, T.LSH[:, k, t, :], T.SG[:, t], True, False)
-            p_e = mm(o, T.LSH[:, k, t, :], T.EB[:, t], False, True)
-    need("v", c_wh)
-    c_hh = ts(T.HH[:, 0:512], T.WH[:, 0:512].indirect(T.LST[:, 0, 0:32]), 1.0 / 512.0, OP.mult)
-    need("s", s_wh)
-    s_hh = scopy(T.HH[:, 512:1024], T.WH[:, 512:1024].indirect(T.LST[:, 0, 32:64]), scale=1.0 / 512.0)
-    need("t", c_hh, s_hh)
-    mm(T.PTT[:, 0, :], T.ONE[0:1, :], T.XR[0:1, :], True, False)
-    for b in range(8):
-        p_ta = mm(T.PTT[:, 0, :], T.DG[:, b, :], T.HH[:, 128 * b:128 * b + 128], False, b == 7)
-    need("v", p_pw)
-    c_pw = vcopy(T.PW[:], T.PWB[:, 128:256])
-    need("v", c_kp, k_key)
-    a = ts(T.TU[:], T.KEY[:], T.KP[:], OP.is_gt)
-    c_mk = ts(T.MK[:], T.J16[:, 0:64], q_, OP.is_equal)
-    need("v", a)
-    c_tri = tt(T.TRI[:], T.TU[:], T.BO[:], OP.mult)
+    s_sg = act(T.SG[:, :, 1, :], T.XB[:], ACT.Sign, bias=-255.5)
+    need("t", c_eb, s_sg)
+    for u in range(2):
+        for i, tab in enumerate((T.EB, T.SG)):
+            for h in range(2):
+                p_e = mm(T.PE0[:, 256 * u:256 * u + 256], T.LS[:, u, h, 2:130], tab[:, h], i + h == 0, i + h == 2)
 
-    def fold(e, lst, win, c):
-        for i in lst:
+    xr = T.IW[:, 0:128]
+
+    def fold(e, ranks, win):
+        c = None
+        for i in ranks:
             need(e, arrive("e1", i))
             o = T.FB[:, 128 * i:128 * i + 128]
             c = (vcopy if e == "v" else scopy)(o, win.indirect(slot_l(i)))
@@ -355,119 +336,112 @@ def rank_program(g, core, T, topo):
     def look(out, win, by, *toks):
         need("v", *toks)
         return vcopy(out, win.indirect(by))
-    need("v", c_pw, k_ir)
-    need("s", k_ir)
+    need("v", c_pw)
     if rank == 0:
         st = vcopy(T.S0[:, 0:1], T.PW[:, 0:1])
     else:
         by = T.LL[:, 0:1]
         far = list(range(mine[0] - 1, 0, -1))
         if first:
-            win, c = fold("v", list(range(rank - 1, 0, -1)), T.PW[:], c_pw)
+            win, c = fold("v", list(range(rank - 1, 0, -1)), T.PW[:])
             a = arrive("e1", 0)
         elif j == 0:
-            low, c = fold("s", far[-1:], T.IR[:], k_ir)
-            win, _ = fold("v", far[:-1], T.PW[:], c_pw)
+            low, c = fold("s", far[-1:], xr)
+            win, _ = fold("v", far[:-1], T.PW[:])
             a = look(T.X4[:], low, by, arrive("e1", 0), c)
             by = T.X4[:, 0:1]
         else:
             own = list(range(rank - 1, mine[0] - 1, -1))
             few = len(own) < len(far)
-            mid, c = fold("s", far[:-1] if few else far, T.IR[:], k_ir)
-            win, _ = fold("v", own, T.PW[:], c_pw)
+            mid, c = fold("s", far[:-1] if few else far, xr)
+            win, _ = fold("v", own, T.PW[:])
             a = arrive("e1", 0)
             if few:
-                low, _ = fold("v", far[-1:], T.IR[:], k_ir)
+                low, _ = fold("v", far[-1:], xr)
                 a = look(T.X1[:], low, by, a)
                 by = T.X1[:, 0:1]
             a = look(T.X4[:], mid, by, a, c)
             by = T.X4[:, 0:1]
         st = look(T.S0[:], win, by, a)
     need("s", p_e)
-    s_ew = act(T.EW[:], T.PE0[:], ACT.Relu, scale=64.0, bias=-63.0)
-    need("v", p_tt, p_ta, k_kc, st)
-    a = ts(T.TA[:, 0, :], T.PTT[:, 0, :], T.S0[:, 0:1], OP.subtract, 512.0, OP.mult)
+    s_ew = act(T.EW[:], T.PE0[:], ACT.Relu, scale=64.0, bias=-223.0)
+
+    def near(i, a):
+        need("v", a)
+        return reduce_(T.RA[:, i:i + 1], T.TA[:, i, :], OP.min, apply_absolute_value=True)
+    need("v", p_t, st, k_nb)
+    a = ts(T.TA[:, 0, :], T.PT[:, 0, :], T.S0[:, 0:1], OP.subtract, 512.0, OP.mult)
     b = ts(T.S1[:], T.S0[:, 0:1], T.M1[:], OP.mult)
+    a = near(0, a)
+    need("v", b)
+    b = ts(T.KB[:], T.KC[:, 0:2], 65536.0, OP.mult, T.S1[:], OP.add)
     need("v", a)
-    a = did("v", V.tensor_reduce(T.RA[:], T.TA[:, 0, :], AX.X, OP.min, apply_absolute_value=True))
-    need("v", a, b)
-    st = ts(T.ST[:, 0:1], T.RA[:], T.MU[:], OP.mult, T.S1[:], OP.add)
-    need("v", st)
-    a = ts(T.TA[:, 1, :], T.PTT[:, 1, :], T.ST[:, 0:1], OP.subtract, 512.0, OP.mult)
-    ts(T.OFP[:, 0:2], T.KC[:, 0:2], T.ST[:, 0:1], OP.add)
+    a = ts(T.TA[:, 1, :], T.PT[:, 1, :], T.RA[:, 0:1], OP.subtract, T.MU[:], OP.mult)
+    a = near(1, a)
     need("v", a)
-    st = did("v", V.tensor_reduce(T.ST[:, 1:2], T.TA[:, 1, :], AX.X, OP.min, apply_absolute_value=True))
-    need("v", st)
-    c_of = ts(T.OFP[:, 2:4], T.KC[:, 2:4], T.ST[:, 1:2], OP.add)
-    need("v", c_of, s_ew, c_mk)
+    a = ts(T.TA[:, 2, :], T.PT[:, 2, :], T.RA[:, 1:2], OP.subtract, T.S1[:], OP.subtract)
+    ts(T.OFP[:, 0:2], T.KB[:], T.RA[:, 1:2], OP.add, 1.0 / 512.0, OP.mult)
+    a = near(2, a)
+    need("v", a)
+    c_of = ts(T.OFP[:, 2:4], T.KC[:, 2:4], T.RA[:, 2:3], OP.add)
+    need("v", c_of, s_ew, s_mk)
+    a = tt(T.FL[:, 0:64], T.EW[:].indirect(T.OFP[:]), T.MKI[:], OP.is_gt)
     c_gv = tt(T.GV[:], T.EW[:].indirect(T.OFP[:]), T.MK[:], OP.mult)
-    need("v", c_gv)
-    a = ts(T.FL[:], T.GV[:], 0.0, OP.is_gt)
     need("v", a)
-    c_inc = scan(T.INC[:], T.ONE[:, 0:64], T.FL[:], OP.mult, OP.add)
-    need("t", c_inc, c_tri, s_w3, c_wh)
-    p_b = mm(T.PSO[:, 0:1], T.TRI[:], T.INC[:, 63:64])
-    p_n = mm(T.PWA[:, 0:1], T.BO[:], T.INC[:, 63:64])
-    need("v", k_rst)
+    c_inc = scan(T.INC[:], T.ONE[:, 0:68], T.FL[:], OP.mult, OP.add)
+    need("t", c_inc, k_tri)
+    mm(T.PSO[:, 0:4], T.TRI[:], T.INC[:, 64:68], True, False)
+    p_b = mm(T.PSO[:, 0:4], T.ID[:], T.INC[:, 15:64:16], False, True)
+    p_n = mm(T.PN[:, 0:1], T.BO[:], T.INC[:, 64:65])
+    need("v", k_rst, c_gv)
     c_scn = scan(T.SCN[:], T.RST[:], T.GV[:], OP.mult, OP.add)
-    need("v", p_b, c_inc)
-    c_pos = ts(T.POS[:], T.INC[:, 15:64:16], T.PSO[:, 0:1], OP.add)
     need("s", p_n, k_nb)
-    s_n = scopy(T.NB[:, 8 * rank:8 * rank + 1], T.PWA[:, 0:1])
+    s_n = scopy(T.NB[:, 8 * rank:8 * rank + 1], T.PN[:, 0:1])
+    s_own = scopy(T.OWN[:], T.PN[:, 0:1])
+    s_b1 = scopy(T.B1[:], T.PN[:, 0:1], scale=-1.0, bias=64.0)
     if rank + 1 < NR:
         need("q", s_n)
         send("en", later(rank), T.NB[:, 8 * rank:8 * rank + 8], lambda d: T.NB[:, 8 * rank:8 * rank + 8])
-    need("s", c_scn)
-    s_nv = scopy(T.NV[:], T.SCN[:, 15:64:16], scale=-1.0)
-    need("s", c_pos, k_io1)
-    a = act(T.OD[:], T.IO1[:], ACT.Abs, scale=-1.0, bias=T.POS[:, 3:4])
-    need("s", a, s_nv)
-    s_oh = act(T.OH[:, 3, :], T.OD[:], ACT.Relu, scale=T.NV[:, 3:4], bias=T.SCN[:, 63:64])
-    s_own = scopy(T.OWN[:], T.PWA[:, 0:1])
-    need("v", c_pos, c_scn, k_io1)
+    need("v", p_b, c_scn)
+    need("t", c_ofs)
     for i in range(4):
-        if i < 3:
-            a = ts(T.OH[:, i, :], T.IO1[:], T.POS[:, i:i + 1], OP.is_equal, T.SCN[:, 16 * i + 15:16 * i + 16], OP.mult)
-        need("t", a if i < 3 else s_oh)
+        a = ts(T.OH[:, i, :], T.IW[:, 1:65], T.PSO[:, i:i + 1], OP.is_equal, T.SCN[:, 16 * i + 15:16 * i + 16], OP.mult)
+        need("t", a)
         p_a = mm(T.PSA[:, 256:320], T.BO[:], T.OH[:, i, :], i == 0, i == 3)
-    a = c_qi = ts(T.QI[:], T.IR[:, 0:17:16], q_, OP.add, float(32 * rank), OP.add)
+    lo = 0 if rank > 0 else 64
+    hi = 192 if rank + 2 < NR else 144 if rank + 1 < NR else 128
+    c_ql = ts(T.QL[:], T.QI[:], float(64 - lo), OP.add)
+    need("v", s_own)
+    c_qo = ts(T.QO[:], T.QI[:], T.OWN[:], OP.subtract)
     need("v", p_a)
     c_a = ts(T.F[:, 64:128], T.PSA[:, 256:320], -1.0, OP.add)
     need("q", c_a)
     n = 64 if rank + 1 < NR else 16
     send("ev", beside(rank), T.F[:, 64:64 + n], lambda d: T.F[:, 0:n] if d > rank else T.F[:, 128:128 + n])
 
-    lo = 0 if rank > 0 else 64
-    hi = 192 if rank + 2 < NR else 144 if rank + 1 < NR else 128
-    u = T.QI[:]
-    need("v", s_own)
-    c_b1 = ts(T.B1[:], T.OWN[:], -1.0, OP.mult, 64.0, OP.add)
+    parts = [T.QL]
+    beg = 0.0
+    need("v", s_b1, c_qo)
     if rank > 0:
         for i in range(rank):
             need("v", arrive("en", i))
-        b = did("v", V.tensor_reduce(T.BEG[:], T.NB[:, 0:8 * rank - 7:8], AX.X, OP.add))
-        c_a1 = ts(T.A1[:], T.NB[:, 8 * rank - 8:8 * rank - 7], 64.0, OP.subtract)
-        need("v", b, c_qi)
-        u = T.U[:]
-        a = ts(u, T.QI[:], T.BEG[:], OP.subtract)
-    need("v", a)
-    o = u
-    if rank + 1 < NR:
-        need("v", c_b1)
-        b = ts(T.U1[:], u, T.OWN[:], OP.is_ge, T.B1[:], OP.mult)
-    if rank > 0:
-        need("v", c_a1)
-        c = ts(T.U3[:], u, 0.0, OP.is_lt, T.A1[:], OP.mult)
-    if rank + 1 < NR:
+        b = reduce_(T.BEG[:], T.NB[:, 0:8 * rank - 7:8], OP.add)
+        c = ts(T.A1[:], T.NB[:, 8 * rank - 8:8 * rank - 7], 64.0, OP.subtract)
         need("v", b)
-        o = T.U2[:]
-        a = tt(o, u, T.U1[:], OP.add)
+        beg = T.BEG[:]
+        ts(T.U[:], T.QL[:], beg, OP.subtract)
+        parts = [T.U]
+    if rank + 1 < NR:
+        a = ts(T.U1[:], T.QO[:], beg, OP.is_ge, T.B1[:], OP.mult)
+        parts.append(T.U1)
     if rank > 0:
-        need("v", a, c)
-        a = tt(T.U4[:], o, T.U3[:], OP.add)
-        o = T.U4[:]
+        need("v", c)
+        a = ts(T.U3[:], T.QI[:], beg, OP.is_lt, T.A1[:], OP.mult)
+        parts.append(T.U3)
     need("v", a)
-    a = ts(T.OF2[:], o, float(64 - lo), OP.add)
+    for i in range(2):
+        x = [p[:, i:i + 1] for p in parts]
+        a = ts(T.OF2[:, i:i + 1], x[0], x[1], OP.add, *((x[2], OP.add) if len(x) > 2 else ()))
     for i in beside(rank):
         need("v", arrive("ev", i))
     need("v", a, c_a)

@@ -3,18 +3,19 @@ from concourse.mybir import dt, AluOpType, AxisListType, ActivationFunctionType
 
 _BUF = {
     "int32": "PI:1 CI:5 SYH:16 SYN:2 X:2x128 XA:2x128 EM:2x128 EI0:2x128",
-    "uint16": "OFS:16 LST:256 LA:32 LB:16 LC:8 LL:64 X1:16 X4:16 OFP:4 OF2:2",
-    "float32": "CF:5 MS:4 CORR:1 SYF:2 MU:1 M1:1 LO:1 HI:1 KC:4 KB:2 S0:16 S1:1 RA:3 TA:3x128 OWN:1 BEG:1 A1:1 B1:1 "
+    "uint16": "OFS:16 LST:256 LA:32 LB:16 LC:8 LR:16 LL:64 X1:16 X4:16 OFX:4 OFP:4 OF2:2",
+    "float32": "CF:5 MS:4 CORR:1 SYF:2 LO:1 HI:1 KC:4 KB:4 S0:16 RA:1 TA:128 OWN:1 BEG:1 A1:1 B1:1 "
                "QI:2 QO:2 QL:2 U:2 U1:2 U3:2 Y1:32 SCN:64",
-    "bfloat16": "ONE:130 IW:256 ID:128 IS:128 R:128 J16:144 SD0:144 SD:128 DG:4x128 X512:128 MK:64 MKI:64 BO1:128 BO:128 "
+    "bfloat16": "ONE:130 IW:256 ID:128 IS:128 R:128 J16:144 SD0:144 SD:128 DG:8x128 X512:128 MKI:64 BO1:128 BO:128 "
+                "T1:256 HH:4x256 HP:4x256 SCR:256 "
                 "TRI:128 RST:64 SYB:16 XI:8x2x16 TL:256 UP:128 LSB:256 ST:64 SEL:2x2x16 LS:2x2x130 W3:4x256 W2:4x256 W1:4x256 "
                 "W0:2x2x256 SCA:512 SCB:256 SCC:128 SCM:128 QM:4x128 HM:256 MM:128 RM:256 ZL:128 ZH:128 PW:128 FB:896 "
-                "XB:2x128 SG:2x2x128 EB:2x2x128 EW:512 GV:64 FL:68 INC:68 OH:4x64 NB:64 F:192",
+                "XB:2x128 XW:256 EB:2x2x128 EW:512 GV:64 FL:68 INC:68 OH:4x64 NB:64 F:192",
 }
 SCRATCH = {n: ("sbuf", [128] + [int(x) for x in d.split("x")], t)
            for t, l in _BUF.items() for n, d in (w.split(":") for w in l.split())}
 for _n, _d in (("PSA", [512]), ("PSD", [512]), ("PZ", [512]), ("PT", [4, 128]), ("PE0", [512]), ("PSO", [512]),
-               ("PN", [512])):
+               ("PN", [512]), ("PX", [512])):
     SCRATCH[_n] = ("psum", [128] + _d, "float32")
 SEMAPHORES = (["v", "s", "t", "q", "dsh", "dsn", "dx0", "dx1", "dem", "dy", "ls"]
               + [p + "_%d" % j for p in ("e1", "en", "ev") for j in range(8)])
@@ -140,19 +141,19 @@ def rank_program(g, core, T, topo):
     need("v", c_one)
     c_xr = scan(T.IW[:, 0:128], T.ONE[:, 0:128], T.ONE[:, 0:128], OP.mult, OP.add, -1.0)
     need("v", k_pi)
-    for i, (sh, m) in enumerate(((5, 15), (0, 255), (6, 3), (5, 1))):
+    for i, (sh, m) in enumerate(((5, 15), (0, 255), (5, 7))):
         a = ts(T.CI[:, i:i + 1], T.PI[:], sh, OP.arith_shift_right, m, OP.bitwise_and)
     need("v", a)
-    c_cf = vcopy(T.CF[:, 0:4], T.CI[:, 0:4])
-    q_, c32, b4, mu = [T.CF[:, i:i + 1] for i in range(4)]
+    c_cf = vcopy(T.CF[:, 0:3], T.CI[:, 0:3])
+    q_, c32, q8 = [T.CF[:, i:i + 1] for i in range(3)]
     c_fl = fill(T.FL[:, 64:68], 0.0)
     need("v", c_cf, c_xr)
-    c_ms = ts(T.MS[:], T.IW[:, 0:4], b4, OP.is_equal)
+    c_ms = ts(T.MS[:], T.IW[:, 0:8:2], q8, OP.is_equal)
     ts(T.CORR[:], q_, 15.0, OP.is_lt, -128.0, OP.mult)
     ts(T.LO[:], q_, 8.0, OP.is_lt, 512.0, OP.mult)
     ts(T.HI[:], q_, 8.0, OP.is_ge, 512.0, OP.mult)
-    ts(T.MU[:], mu, 512.0, OP.mult)
-    ts(T.M1[:], mu, 1.0, OP.is_lt)
+    ts(T.KB[:], T.IW[:, 0:4], 3.0, OP.is_equal, 65536.0, OP.mult)
+    c_qi = ts(T.QI[:], T.IW[:, 0:17:16], q_, OP.add, float(32 * rank), OP.add)
     need("v", k_j16)
     c_sd0 = ts(T.SD0[:], T.J16[:], q_, OP.is_equal, -65536.0, OP.mult)
 
@@ -167,22 +168,21 @@ def rank_program(g, core, T, topo):
     for m in range(4):
         s_dg = scopy(T.DG[:, m, :], T.ID[:], scale=T.MS[:, m:m + 1])
 
+    need("v", dsh)
+    c_syb = vcopy(T.SYB[0:16, :], T.SYH[0:16, :])
+    need("t", c_syb, k_r)
+    p_of = mm(T.PSA[:, 0:16], T.R[0:16, :], T.SYB[0:16, :])
     c_a = []
     for h in range(2):
         need("v", dx[h])
         c_a.append(ts(T.XA[:, h, :], T.X[:, h, :], 127, OP.bitwise_and))
-        if h == 0:
-            need("v", dsh)
-            c_syb = vcopy(T.SYB[0:16, :], T.SYH[0:16, :])
-            need("t", c_syb, k_r)
-            p_of = mm(T.PSA[:, 0:16], T.R[0:16, :], T.SYB[0:16, :])
     for h in range(2):
         need("v", c_a[h])
         c_xi = vcopy(T.XI[:, :, h, :], T.XA[:, h, :])
-    need("v", dsn)
-    c_syf = vcopy(T.SYF[:], T.SYN[:])
     need("v", p_of)
     c_ofs = ts(T.OFS[:], T.PSA[:, 0:16], c32, OP.add)
+    need("v", dsn)
+    c_syf = vcopy(T.SYF[:], T.SYN[:])
     need("v", c_xi)
     c_tl = did("v", V.transpose(T.TL[:], T.XI[:]))
     need("v", c_syf)
@@ -195,7 +195,6 @@ def rank_program(g, core, T, topo):
         need("v", c_l[e])
         c_l[e] = vcopy(T.LST[:, 128 * e:128 * e + 128], T.LSB[:, 128 * e:128 * e + 128])
         if e == 0:
-            need("v", c_st)
             c_sel = did("v", V.transpose(T.SEL[:], T.ST[:]))
 
     need("q", c_sel, s_z)
@@ -206,23 +205,23 @@ def rank_program(g, core, T, topo):
             k_ls = where(T.LS[32 * a:32 * a + 32, :, h, o:o + 16], T.SEL[32 * a:32 * a + 32, :, h, :], [[0, 32]],
                          OP.is_equal, 0, 0)
     need("q", k_ls)
-    iota(T.KC[:, 0:2], [[1, 2]])
-    iota(T.KC[:, 2:4], [[128, 2]], 0, 256)
-    k_nb = iota(T.NB[:, 8 * rank:8 * rank + 8], [[0, 8]])
-    need("q", k_bo)
-    k_tri = where(T.TRI[:], T.BO[:], [[1, 128]], OP.is_gt, 0, -1)
+    for m in range(4):
+        k_dg = where(T.DG[:, 4 + m, :], T.ID[:], [[0, 16], [1, 8]], OP.is_equal, -2 * m - 1, 0)
+    need("q", *dx)
+    k_xb = where(T.XB[:], T.X[:], [[0, 256]], OP.is_equal, 0, 0)
     need("t", c_sd0, k_id, s_is)
     mm(T.PSD[:, 0:128], T.ID[:], T.SD0[:, 16:144], True, False)
     p_sd = mm(T.PSD[:, 0:128], T.IS[:], T.SD0[:, 15:143], False, True)
     need("s", p_sd)
     s_sd = scopy(T.SD[:], T.PSD[:, 0:128])
-    scopy(T.MK[:], T.SD0[:, 0:64], scale=-1.0 / 65536.0)
-    s_mk = scopy(T.MKI[:], T.SD0[:, 0:64], scale=1.0 / 64.0, bias=1024.0)
-    need("t", k_ls, s_x5, c_xi)
-    for i, (u, o) in enumerate(((0, 1), (1, 1), (0, 2))):
-        mm(T.PT[:, i, :], T.ONE[0:1, 0:128], T.X512[0:1, :], True, False)
-        for h in range(2):
-            p_t = mm(T.PT[:, i, :], T.LS[:, u, h, o:o + 128], T.XI[:, :, h, :], False, h == 1)
+    for i in range(4):
+        s_mk = scopy(T.MKI[:, 16 * i:16 * i + 16], T.SD0[:, 0:16], scale=1.0 / 64.0, bias=1151.0 + 128.0 * (i % 2))
+    need("t", k_ls, s_x5, c_xi, s_sd)
+    for h in range(2):
+        p_t1 = mm(T.PSD[:, 128:256], T.LS[:, 1, h, 1:129], T.XI[:, :, h, :], h == 0, h == 1)
+    mm(T.PT[:, 0, :], T.ONE[0:1, 0:128], T.X512[0:1, :], True, False)
+    for h in range(2):
+        p_t = mm(T.PT[:, 0, :], T.LS[:, 0, h, 2:130], T.XI[:, :, h, :], False, h == 1)
 
     def lst(e, side, k):
         o = 128 * e + 64 * side + 16 * k
@@ -233,14 +232,23 @@ def rank_program(g, core, T, topo):
     tok = {}
     need("v", c_l[0], s_iw)
     need("s", c_l[1], s_iw)
-    for k in (3, 2, 1, 0):
-        for side in range(2):
-            for e, (qu, f) in enumerate((("v", vcopy), ("s", scopy))):
-                win = T.IW[:] if k == 3 else T["W%d" % (k + 1)][:, 2 * e + side, :]
-                out = T.W0[:, e, side, :] if k == 0 else T["W%d" % k][:, 2 * e + side, :]
-                if k < 3:
-                    need(qu, tok[e, side])
-                tok[e, side] = f(out, win.indirect(lst(e, side, k)))
+    for e, qu, f, order in ((1, "s", scopy, (0, 0, 1, 0, 1, 0, 1, 1)), (0, "v", vcopy, (0, 1, 0, 1, 0, 1, 0, 1))):
+        step = [3, 3]
+        for side in order:
+            k = step[side]
+            step[side] -= 1
+            win = T.IW[:] if k == 3 else T["W%d" % (k + 1)][:, 2 * e + side, :]
+            out = T.W0[:, e, side, :] if k == 0 else T["W%d" % k][:, 2 * e + side, :]
+            by = lst(e, side, k)
+            if (k, e, side) == (3, 0, 1):
+                out, by = out[:, 0:128], by[:, 0:8]
+            if (k, e, side) == (2, 0, 1):
+                need(qu, s_5)
+            if k < 3:
+                need(qu, tok[e, side])
+            tok[e, side] = f(out, win.indirect(by))
+            if (k, e, side) == (3, 1, 0):
+                s_5 = scopy(T.W3[:, 1, 128:256], T.IW[:].indirect(lst(0, 1, 3)[:, 8:16]))
 
     def diag(sc, at, win):
         return scan(sc[:, 128 * at:128 * at + 128], T.SD[:], win, OP.add, OP.max)
@@ -264,9 +272,10 @@ def rank_program(g, core, T, topo):
     need("s", l1, tok[1, 1])
     s_q1 = scopy(qm(1), w0(3).indirect(T.LA[:, 16:24]))
     s_q3 = scopy(qm(3), w0(7).indirect(T.LA[:, 24:32]))
+    need("s", p_t1)
+    scopy(T.T1[:, 0:128], T.PSD[:, 128:256])
     need("v", c_q0)
     a = diag(T.SCB, 0, qm(0))
-    c_qi = ts(T.QI[:], T.IW[:, 0:17:16], q_, OP.add, float(32 * rank), OP.add)
     need("v", c_q2)
     b = diag(T.SCB, 1, qm(2))
     need("v", a)
@@ -293,18 +302,53 @@ def rank_program(g, core, T, topo):
         c_lm = pick(slot_l(rank), T.SCM, 0)
         need("q", c_lm)
         send("e1", later(rank), slot_l(rank), lambda d: slot_l(rank))
+    iota(T.KC[:, 0:2], [[0, 2]], 0, 128)
+    iota(T.KC[:, 2:4], [[128, 2]], 0, 256)
+    k_nb = iota(T.NB[:, 8 * rank:8 * rank + 8], [[0, 8]])
+    k_tri = where(T.TRI[:], T.BO[:], [[1, 128]], OP.is_gt, 0, -1)
 
     scopy(T.RM[:, 0:128], w0(2).indirect(T.LB[:, 0:8]))
     s_rm = scopy(T.RM[:, 128:256], w0(6).indirect(T.LB[:, 8:16]))
+    s_t1 = scopy(T.T1[:, 128:256], T.PSD[:, 128:256])
     need("t", s_dg, s_iw, c_q2)
     for m, win in enumerate((T.IW[:], T.W0[:, 0, 0, :], T.QM[:, 0:4:2, :], T.RM[:])):
         if m == 3:
             need("t", s_rm)
-        p_z = mm(T.PZ[:, 0:256], T.DG[:, m, :], win, m == 0, m == 3)
+        mm(T.PZ[:, 0:256], T.DG[:, m, :], win, m == 0, False)
+
+    def half(e, m):
+        need(e, s_t1)
+        return (vcopy if e == "v" else scopy)(T.HH[:, m, :], T.T1[:].indirect(lst(m // 2, m % 2, 0)))
+
+    def onto(e, m, i, by, *toks):
+        need(e, *toks)
+        x = (vcopy if e == "v" else scopy)(T.HP[:, m, 128 * i:128 * i + 128],
+                                           T.HH[:, m, 128 * i:128 * i + 128].indirect(by[:, 8 * i:8 * i + 8]))
+        need("t", x)
+        return mm(T.PZ[:, 128 * i:128 * i + 128], T.DG[:, 4 + m, :], T.HP[:, m, 128 * i:128 * i + 128], False, m + i == 3 and m == 2)
+    need("t", k_xb)
+    for u in range(2):
+        for h in range(2):
+            p_x = mm(T.PX[:, 128 * u:128 * u + 128], T.LS[:, u, h, 2:130], T.XB[:, h, :], h == 0, h == 1)
+    s_h3, s_h2 = half("s", 3), half("s", 2)
+    need("v", s_rm)
+    a = [diag(T.SCR, i, T.RM[:, 128 * i:128 * i + 128]) for i in range(2)][1]
+    c_h1 = half("v", 1)
+    need("v", a)
+    c_lr = pick(T.LR[:], T.SCR, 0, 2)
+    c_h0 = half("v", 0)
+    need("t", k_dg, c_h0)
+    mm(T.PZ[:, 0:256], T.DG[:, 4, :], T.HH[:, 0, :], False, False)
+    for i in range(2):
+        onto("s", 3, i, T.LR, s_h3, c_lr)
+        onto("v", 1, i, T.LA, c_h1)
+    onto("s", 2, 0, T.LB, s_h2)
+    p_z = onto("v", 2, 1, T.LB, s_h2)
+    need("s", p_x)
+    s_xw = scopy(T.XW[:], T.PX[:, 0:256])
     need("s", p_z)
     scopy(T.ZH[:], T.PZ[:, 128:256], scale=T.HI[:])
     s_zl = scopy(T.ZL[:], T.PZ[:, 0:128], scale=T.LO[:])
-    c_xb = vcopy(T.XB[:], T.X[:])
     need("v", dem)
     a = ts(T.EI0[:], T.EM[:], 63, OP.bitwise_and)
     ts(T.EB[:, :, 1, :], T.EM[:], 1.0 / 4096.0, OP.mult, (160.0 - 31.5 / 64.0) / 64.0, OP.add)
@@ -312,14 +356,10 @@ def rank_program(g, core, T, topo):
     c_eb = ts(T.EB[:, :, 0, :], T.EI0[:], 1.0 / 64.0, OP.mult, 2.5, OP.add)
     need("v", s_zl, c_lc)
     c_pw = tt(T.PW[:], T.ZH[:].indirect(T.LC[:]), T.ZL[:], OP.add)
-    need("s", c_xb)
-    act(T.SG[:, :, 0, :], T.XB[:], ACT.Sign, bias=-127.5)
-    s_sg = act(T.SG[:, :, 1, :], T.XB[:], ACT.Sign, bias=-255.5)
-    need("t", c_eb, s_sg)
+    need("t", c_eb)
     for u in range(2):
-        for i, tab in enumerate((T.EB, T.SG)):
-            for h in range(2):
-                p_e = mm(T.PE0[:, 256 * u:256 * u + 256], T.LS[:, u, h, 2:130], tab[:, h], i + h == 0, i + h == 2)
+        for h in range(2):
+            p_e = mm(T.PE0[:, 256 * u:256 * u + 256], T.LS[:, u, h, 2:130], T.EB[:, h], h == 0, h == 1)
 
     xr = T.IW[:, 0:128]
 
@@ -364,31 +404,22 @@ def rank_program(g, core, T, topo):
             by = T.X4[:, 0:1]
         st = look(T.S0[:], win, by, a)
     need("s", p_e)
-    s_ew = act(T.EW[:], T.PE0[:], ACT.Relu, scale=64.0, bias=-223.0)
-
-    def near(i, a):
-        need("v", a)
-        return reduce_(T.RA[:, i:i + 1], T.TA[:, i, :], OP.min, apply_absolute_value=True)
+    s_ew = scopy(T.EW[:], T.PE0[:], scale=64.0, bias=-159.0)
     need("v", p_t, st, k_nb)
-    a = ts(T.TA[:, 0, :], T.PT[:, 0, :], T.S0[:, 0:1], OP.subtract, 512.0, OP.mult)
-    b = ts(T.S1[:], T.S0[:, 0:1], T.M1[:], OP.mult)
-    a = near(0, a)
-    need("v", b)
-    b = ts(T.KB[:], T.KC[:, 0:2], 65536.0, OP.mult, T.S1[:], OP.add)
+    a = ts(T.TA[:], T.PT[:, 0, :], T.S0[:, 0:1], OP.subtract)
+    ts(T.OFX[:, 0:2], T.KB[:, 0:2], T.S0[:, 0:1], OP.add, 1.0 / 512.0, OP.mult)
     need("v", a)
-    a = ts(T.TA[:, 1, :], T.PT[:, 1, :], T.RA[:, 0:1], OP.subtract, T.MU[:], OP.mult)
-    a = near(1, a)
+    a = reduce_(T.RA[:], T.TA[:], OP.min, apply_absolute_value=True)
+    ts(T.OFP[:, 0:2], T.KB[:, 2:4], T.S0[:, 0:1], OP.add, 1.0 / 512.0, OP.mult)
     need("v", a)
-    a = ts(T.TA[:, 2, :], T.PT[:, 2, :], T.RA[:, 1:2], OP.subtract, T.S1[:], OP.subtract)
-    ts(T.OFP[:, 0:2], T.KB[:], T.RA[:, 1:2], OP.add, 1.0 / 512.0, OP.mult)
-    a = near(2, a)
-    need("v", a)
-    c_of = ts(T.OFP[:, 2:4], T.KC[:, 2:4], T.RA[:, 2:3], OP.add)
-    need("v", c_of, s_ew, s_mk)
-    a = tt(T.FL[:, 0:64], T.EW[:].indirect(T.OFP[:]), T.MKI[:], OP.is_gt)
-    c_gv = tt(T.GV[:], T.EW[:].indirect(T.OFP[:]), T.MK[:], OP.mult)
+    a = ts(T.OFX[:, 2:4], T.KC[:, 0:2], T.RA[:], OP.add)
+    c_of = ts(T.OFP[:, 2:4], T.KC[:, 2:4], T.RA[:], OP.add)
+    need("v", a, s_xw, s_mk)
+    a = tt(T.FL[:, 0:64], T.XW[:].indirect(T.OFX[:]), T.MKI[:], OP.is_gt)
     need("v", a)
     c_inc = scan(T.INC[:], T.ONE[:, 0:68], T.FL[:], OP.mult, OP.add)
+    need("v", c_of, s_ew)
+    c_gv = tt(T.GV[:], T.EW[:].indirect(T.OFP[:]), T.FL[:, 0:64], OP.mult)
     need("t", c_inc, k_tri)
     mm(T.PSO[:, 0:4], T.TRI[:], T.INC[:, 64:68], True, False)
     p_b = mm(T.PSO[:, 0:4], T.ID[:], T.INC[:, 15:64:16], False, True)

@@ -2,19 +2,17 @@ from concourse.bass import DstId, RemoteDMATransfer
 from concourse.mybir import dt, AluOpType, AxisListType, ActivationFunctionType
 
 _BUF = {
-    "int32": "PI:1 CI:5 SYH:16 SYN:2 X:2x128 XA:2x128 EM:2x128 EI0:2x128",
-    "uint16": "OFS:16 LST:256 LA:32 LB:16 LC:8 LR:16 LL:64 X1:16 X4:16 OFX:4 OFP:4 OF2:2",
-    "float32": "CF:5 MS:4 CORR:1 SYF:2 LO:1 HI:1 KC:4 KB:4 S0:16 RA:1 TA:128 OWN:1 BEG:1 A1:1 B1:1 "
-               "QI:2 QO:2 QL:2 U:2 U1:2 U3:2 Y1:32 SCN:64",
-    "bfloat16": "ONE:130 IW:256 ID:128 IS:128 R:128 J16:144 SD0:144 SD:128 DG:8x128 X512:128 MKI:64 BO1:128 BO:128 "
-                "T1:256 HH:4x256 HP:4x256 SCR:256 "
-                "TRI:128 RST:64 SYB:16 XI:8x2x16 TL:256 UP:128 LSB:256 ST:64 SEL:2x2x16 LS:2x2x130 W3:4x256 W2:4x256 W1:4x256 "
-                "W0:2x2x256 SCA:512 SCB:256 SCC:128 SCM:128 QM:4x128 HM:256 MM:128 RM:256 ZL:128 ZH:128 PW:128 FB:896 "
+    "int32": "PI:1 CI:4 SYH:16 SYN:2 X:2x128 XA:2x128 EM:2x128 EI0:2x128",
+    "uint16": "OFS:16 LST:256 LB:16 LC:8 LL:64 X1:16 X4:16 OFX:16 OFP:4 OF2:2",
+    "float32": "CF:4 MS:4 TM:4 CORR:1 SYF:2 LO:1 HI:1 KC:4 RA:16 OWN:1 BEG:1 A1:1 B1:1 QI:2 QO:1 QL:2 U:2 Y1:32 SCN:64",
+    "bfloat16": "ONE:130 IW:128 ID:128 IS:128 R:128 J16:144 SD0:144 SD:128 DG:4x128 T0:128 TA:16 MKI:64 BO1:128 BO:128 "
+                "TRI:128 RST:32 SYB:16 XI:8x2x16 TL:256 ST:64 SEL:2x2x16 LS:2x2x130 W:32x128 SCB:256 SCC:128 SCM:128 "
+                "HM:256 MM:128 TR:4x128 P:32x128 PB:2x128 ZL:128 ZH:128 PW:128 FB:896 "
                 "XB:2x128 XW:256 EB:2x2x128 EW:512 GV:64 FL:68 INC:68 OH:4x64 NB:64 F:192",
 }
 SCRATCH = {n: ("sbuf", [128] + [int(x) for x in d.split("x")], t)
            for t, l in _BUF.items() for n, d in (w.split(":") for w in l.split())}
-for _n, _d in (("PSA", [512]), ("PSD", [512]), ("PZ", [512]), ("PT", [4, 128]), ("PE0", [512]), ("PSO", [512]),
+for _n, _d in (("PSA", [512]), ("PSD", [512]), ("PZ", [512]), ("PT", [512]), ("PE0", [512]), ("PSO", [512]),
                ("PN", [512]), ("PX", [512])):
     SCRATCH[_n] = ("psum", [128] + _d, "float32")
 SEMAPHORES = (["v", "s", "t", "q", "dsh", "dsn", "dx0", "dx1", "dem", "dy", "ls"]
@@ -29,7 +27,6 @@ def rank_program(g, core, T, topo):
     NR = len(T.cores)
     mine = [r for r, c in enumerate(T.cores) if topo.chip(c) == topo.chip(core)]
     j = mine.index(rank)
-    first = mine[0] == 0
     Q = {"v": g.vector, "s": g.scalar, "t": g.tensor, "q": g, "y": g.sync}
     cnt = {"v": 0, "s": 0, "t": 0, "q": 0}
     seen = {}
@@ -72,6 +69,10 @@ def rank_program(g, core, T, topo):
     def scopy(out, in_, **k):
         return act(out, in_, ACT.Copy, **k)
 
+    def gather(e, out, win, by, *toks):
+        need(e, *toks)
+        return (vcopy if e == "v" else scopy)(out, win.indirect(by))
+
     def mm(out, lhsT, rhs, start=True, stop=True):
         return did("t", PE.matmul(out, lhsT, rhs, start, stop))
 
@@ -84,15 +85,20 @@ def rank_program(g, core, T, topo):
     def same(r, r2):
         return topo.chip(T.cores[r]) == topo.chip(T.cores[r2])
 
-    def plan(r, dsts):
+    def plan(kind, r, dsts):
         near, far = [d for d in dsts if same(r, d)], [d for d in dsts if not same(r, d)]
         p = []
         if near:
             es = topo.engines(T.cores[r], T.cores[near[0]])
+            out = topo.engines(T.cores[r], T.cores[[d for d in range(NR) if not same(r, d)][0]])
             if far or r + 1 == NR:
-                other = [d for d in range(NR) if not same(r, d)][0]
-                es = [e for e in es if e not in topo.engines(T.cores[r], T.cores[other])]
+                es = [e for e in es if e not in out]
             p.append((near, es))
+        if kind == "e1":
+            near.sort()
+            far = [sorted(far)[(r + k) % len(far)] for k in range(len(far))]
+        if kind == "en":
+            far.sort()
         if far:
             p.append((far, topo.engines(T.cores[r], T.cores[far[0]])))
         return p
@@ -105,12 +111,12 @@ def rank_program(g, core, T, topo):
 
     def arrive(kind, r):
         dsts = beside(r) if kind == "ev" else later(r)
-        return ("%s_%d" % (kind, r), [len(es) for ds, es in plan(r, dsts) if rank in ds][0])
+        return ("%s_%d" % (kind, r), [len(es) for ds, es in plan(kind, r, dsts) if rank in ds][0])
     sent = [0]
 
     def send(kind, dsts, src_, at):
         trs = []
-        for ds, es in plan(rank, dsts):
+        for ds, es in plan(kind, rank, dsts):
             adr = [topo.addr(T.cores[d]) for d in ds]
             trs.append(RemoteDMATransfer(dst_ids=[DstId(rid=x[0], pnc=x[1]) for x in adr],
                                          dma_engine_mask=sum(1 << e for e in es),
@@ -121,48 +127,40 @@ def rank_program(g, core, T, topo):
     g.sync.dma_start(T.X[:, 0, :], T.nx[0:8:2, :]).then_inc(T.sem.dx0, 16)
     S.dma_start(T.SYH[0:16, :], T.sy[:, :]).then_inc(T.sem.dsh, 16)
     S.dma_start(T.X[:, 1, :], T.nx[1:8:2, :]).then_inc(T.sem.dx1, 16)
-    g.sync.dma_start(T.SYN[:], T.sy[:, :]).then_inc(T.sem.dsn, 16)
+    S.dma_start(T.SYN[:], T.sy[:, :]).then_inc(T.sem.dsn, 16)
+    dsh, dsn, dx, dem = ("dsh", 16), ("dsn", 16), [("dx0", 16), ("dx1", 16)], ("dem", 32)
+    need("y", dx[1])
     g.sync.dma_start(T.EM[:, 0, :], T.em[0:8:2, :]).then_inc(T.sem.dem, 16)
     g.sync.dma_start(T.EM[:, 1, :], T.em[1:8:2, :]).then_inc(T.sem.dem, 16)
-    dsh, dsn, dx, dem = ("dsh", 16), ("dsn", 16), [("dx0", 16), ("dx1", 16)], ("dem", 32)
 
     c_one = fill(T.ONE[:], 1.0)
     k_pi = did("q", g.iota(T.PI[:], [[0, 1]], 0, 32))
     need("q", c_one)
     k_r = where(T.R[0:16, :], T.ONE[0:16, 0:128], [[1, 16], [0, 8]], OP.is_equal, 0, -1)
     k_j16 = iota(T.J16[:], [[0, 9], [1, 16]])
-    k_up = iota(T.UP[:], [[0, 8], [128, 2], [0, 8]])
     k_id = where(T.ID[:], T.ONE[:, 0:128], [[-1, 128]], OP.is_equal, 0, 1)
-    k_bo1 = where(T.BO1[:], T.ONE[:, 0:128], [[-16, 8], [0, 16]], OP.is_ge, 0, 1)
-    k_rst = where(T.RST[:], T.ONE[:, 0:64], [[0, 4], [1, 16]], OP.not_equal, 0, 0)
-    need("q", k_bo1)
-    k_bo = where(T.BO[:], T.BO1[:], [[16, 8], [0, 16]], OP.is_ge, 15, -1)
 
     need("v", c_one)
     c_xr = scan(T.IW[:, 0:128], T.ONE[:, 0:128], T.ONE[:, 0:128], OP.mult, OP.add, -1.0)
+    xr = T.IW[:, 0:128]
     need("v", k_pi)
-    for i, (sh, m) in enumerate(((5, 15), (0, 255), (5, 7))):
+    for i, (sh, m) in enumerate(((5, 15), (0, 255), (5, 7), (5, 3))):
         a = ts(T.CI[:, i:i + 1], T.PI[:], sh, OP.arith_shift_right, m, OP.bitwise_and)
     need("v", a)
-    c_cf = vcopy(T.CF[:, 0:3], T.CI[:, 0:3])
-    q_, c32, q8 = [T.CF[:, i:i + 1] for i in range(3)]
+    c_cf = vcopy(T.CF[:], T.CI[:])
+    q_, c32, q8, q4 = [T.CF[:, i:i + 1] for i in range(4)]
     c_fl = fill(T.FL[:, 64:68], 0.0)
     need("v", c_cf, c_xr)
-    c_ms = ts(T.MS[:], T.IW[:, 0:8:2], q8, OP.is_equal)
+    ts(T.MS[:, 0:2], T.IW[:, 0:8:4], q8, OP.is_equal)
+    ts(T.MS[:, 2:3], q8, 4.0, OP.is_lt)
+    c_ms = ts(T.MS[:, 3:4], q8, 4.0, OP.is_ge)
     ts(T.CORR[:], q_, 15.0, OP.is_lt, -128.0, OP.mult)
-    ts(T.LO[:], q_, 8.0, OP.is_lt, 512.0, OP.mult)
-    ts(T.HI[:], q_, 8.0, OP.is_ge, 512.0, OP.mult)
-    ts(T.KB[:], T.IW[:, 0:4], 3.0, OP.is_equal, 65536.0, OP.mult)
-    c_qi = ts(T.QI[:], T.IW[:, 0:17:16], q_, OP.add, float(32 * rank), OP.add)
-    need("v", k_j16)
-    c_sd0 = ts(T.SD0[:], T.J16[:], q_, OP.is_equal, -65536.0, OP.mult)
+    ts(T.TM[:], T.IW[:, 0:4], q4, OP.is_equal)
 
     need("s", c_one, c_xr)
     for u in range(2):
         for h in range(2):
             s_z = scopy(T.LS[:, u, h, :], T.ONE[:], scale=0.0)
-    s_iw = scopy(T.IW[:, 128:256], T.IW[:, 0:128])
-    s_x5 = scopy(T.X512[0:1, :], T.IW[0:1, 0:128], scale=512.0)
     need("s", k_id, c_ms)
     s_is = scopy(T.IS[:], T.ID[:], scale=-1.0 / 512.0)
     for m in range(4):
@@ -176,6 +174,9 @@ def rank_program(g, core, T, topo):
     for h in range(2):
         need("v", dx[h])
         c_a.append(ts(T.XA[:, h, :], T.X[:, h, :], 127, OP.bitwise_and))
+        if h == 0:
+            need("v", k_j16)
+            c_sd0 = ts(T.SD0[:], T.J16[:], q_, OP.is_equal, -65536.0, OP.mult)
     for h in range(2):
         need("v", c_a[h])
         c_xi = vcopy(T.XI[:, :, h, :], T.XA[:, h, :])
@@ -188,14 +189,9 @@ def rank_program(g, core, T, topo):
     need("v", c_syf)
     for u in range(2):
         c_st = ts(T.ST[:, 32 * u:32 * u + 32], T.IW[:, 0:32], T.SYF[:, u:u + 1], OP.is_equal)
-    need("v", c_tl, c_ofs, k_up)
-    c_l = [tt(T.LSB[:, 128 * e:128 * e + 128], T.TL[:].indirect(T.OFS[:, 8 * e:8 * e + 8]), T.UP[:], OP.add)
-           for e in range(2)]
-    for e in range(2):
-        need("v", c_l[e])
-        c_l[e] = vcopy(T.LST[:, 128 * e:128 * e + 128], T.LSB[:, 128 * e:128 * e + 128])
-        if e == 0:
-            c_sel = did("v", V.transpose(T.SEL[:], T.ST[:]))
+    c_l = {e: gather("v", T.LST[:, 128 * e:128 * e + 128], T.TL[:], T.OFS[:, 8 * e:8 * e + 8], c_tl, c_ofs) for e in (0, 1)}
+    need("v", c_st)
+    c_sel = did("v", V.transpose(T.SEL[:], T.ST[:]))
 
     need("q", c_sel, s_z)
     for a in range(4):
@@ -204,228 +200,236 @@ def rank_program(g, core, T, topo):
             o = 2 + 32 * a + 16 * h
             k_ls = where(T.LS[32 * a:32 * a + 32, :, h, o:o + 16], T.SEL[32 * a:32 * a + 32, :, h, :], [[0, 32]],
                          OP.is_equal, 0, 0)
-    need("q", k_ls)
-    for m in range(4):
-        k_dg = where(T.DG[:, 4 + m, :], T.ID[:], [[0, 16], [1, 8]], OP.is_equal, -2 * m - 1, 0)
-    need("q", *dx)
+    need("q", k_ls, *dx)
     k_xb = where(T.XB[:], T.X[:], [[0, 256]], OP.is_equal, 0, 0)
     need("t", c_sd0, k_id, s_is)
     mm(T.PSD[:, 0:128], T.ID[:], T.SD0[:, 16:144], True, False)
     p_sd = mm(T.PSD[:, 0:128], T.IS[:], T.SD0[:, 15:143], False, True)
     need("s", p_sd)
     s_sd = scopy(T.SD[:], T.PSD[:, 0:128])
-    for i in range(4):
-        s_mk = scopy(T.MKI[:, 16 * i:16 * i + 16], T.SD0[:, 0:16], scale=1.0 / 64.0, bias=1151.0 + 128.0 * (i % 2))
-    need("t", k_ls, s_x5, c_xi, s_sd)
+    for i in range(2):
+        s_mk = scopy(T.MKI[:, 16 * i:16 * i + 16], T.SD0[:, 0:16], scale=1.0 / 64.0, bias=1151.0 + 128.0 * i)
+    need("t", k_ls, c_xi, s_sd)
     for h in range(2):
         p_t1 = mm(T.PSD[:, 128:256], T.LS[:, 1, h, 1:129], T.XI[:, :, h, :], h == 0, h == 1)
-    mm(T.PT[:, 0, :], T.ONE[0:1, 0:128], T.X512[0:1, :], True, False)
     for h in range(2):
-        p_t = mm(T.PT[:, 0, :], T.LS[:, 0, h, 2:130], T.XI[:, :, h, :], False, h == 1)
+        p_t = mm(T.PT[:, 0:128], T.LS[:, 0, h, 2:130], T.XI[:, :, h, :], h == 0, h == 1)
+    need("t", k_xb)
+    for u in range(2):
+        for h in range(2):
+            p_x = mm(T.PX[:, 128 * u:128 * u + 128], T.LS[:, u, h, 2:130], T.XB[:, h, :], h == 0, h == 1)
 
-    def lst(e, side, k):
-        o = 128 * e + 64 * side + 16 * k
-        return T.LST[:, o:o + 16]
-
-    def w0(b):
-        return T.W0[:, b % 4 // 2, b % 2, 128 * (b // 4):128 * (b // 4) + 128]
-    tok = {}
-    need("v", c_l[0], s_iw)
-    need("s", c_l[1], s_iw)
-    for e, qu, f, order in ((1, "s", scopy, (0, 0, 1, 0, 1, 0, 1, 1)), (0, "v", vcopy, (0, 1, 0, 1, 0, 1, 0, 1))):
-        step = [3, 3]
-        for side in order:
-            k = step[side]
-            step[side] -= 1
-            win = T.IW[:] if k == 3 else T["W%d" % (k + 1)][:, 2 * e + side, :]
-            out = T.W0[:, e, side, :] if k == 0 else T["W%d" % k][:, 2 * e + side, :]
-            by = lst(e, side, k)
-            if (k, e, side) == (3, 0, 1):
-                out, by = out[:, 0:128], by[:, 0:8]
-            if (k, e, side) == (2, 0, 1):
-                need(qu, s_5)
-            if k < 3:
-                need(qu, tok[e, side])
-            tok[e, side] = f(out, win.indirect(by))
-            if (k, e, side) == (3, 1, 0):
-                s_5 = scopy(T.W3[:, 1, 128:256], T.IW[:].indirect(lst(0, 1, 3)[:, 8:16]))
+    def lst(k):
+        o = 16 * (k % 16) + 8 * (k // 16)
+        return T.LST[:, o:o + 8]
+    tok = {0: c_l[0], 1: c_l[1], 2: c_l[0], 3: c_l[1]}
+    for i in range(7, -1, -1):
+        for b in range(4):
+            k = 8 * b + i
+            tok[b] = gather("s" if k == 7 else "vs"[b % 2], T.W[:, k, :], xr if i == 7 else T.W[:, k + 1, :], lst(k), tok[b])
 
     def diag(sc, at, win):
         return scan(sc[:, 128 * at:128 * at + 128], T.SD[:], win, OP.add, OP.max)
 
-    def pick(out, sc, at, n=1):
-        return ts(out, sc[:, 128 * at + 15:128 * (at + n):16], T.CORR[:], OP.add)
+    def pick(out, sc, at):
+        return ts(out, sc[:, 128 * at + 15:128 * at + 128:16], T.CORR[:], OP.add)
 
-    def qm(b):
-        return T.QM[:, b, :]
-    d = []
-    for i, b in enumerate((0, 4, 2, 6)):
-        need("v", tok[i // 2, 0], s_sd)
-        d.append(diag(T.SCA, i, w0(b)))
-    need("v", d[1])
-    l0 = pick(T.LA[:, 0:16], T.SCA, 0, 2)
-    need("v", d[3])
-    l1 = pick(T.LA[:, 16:32], T.SCA, 2, 2)
-    need("v", l0, tok[0, 1])
-    c_q0 = vcopy(qm(0), w0(1).indirect(T.LA[:, 0:8]))
-    c_q2 = vcopy(qm(2), w0(5).indirect(T.LA[:, 8:16]))
-    need("s", l1, tok[1, 1])
-    s_q1 = scopy(qm(1), w0(3).indirect(T.LA[:, 16:24]))
-    s_q3 = scopy(qm(3), w0(7).indirect(T.LA[:, 24:32]))
-    need("s", p_t1)
-    scopy(T.T1[:, 0:128], T.PSD[:, 128:256])
-    need("v", c_q0)
-    a = diag(T.SCB, 0, qm(0))
-    need("v", c_q2)
-    b = diag(T.SCB, 1, qm(2))
+    def low(h):
+        return ts(T.EI0[:, h, :], T.EM[:, h, :], 63, OP.bitwise_and)
+
+    def high(h):
+        return ts(T.EB[:, h, 1, :], T.EM[:, h, :], 1.0 / 4096.0, OP.mult, (160.0 - 31.5 / 64.0) / 64.0, OP.add)
+    need("v", tok[0], s_sd)
+    a = diag(T.SCB, 0, T.W[:, 0, :])
+    need("v", p_t1)
+    s_tr = {3: ts(T.TR[:, 3, :], T.PSD[:, 128:256], T.TM[:, 3:4], OP.mult)}
+    need("v", tok[2])
+    b = diag(T.SCB, 1, T.W[:, 16, :])
     need("v", a)
     c_b0 = pick(T.LB[:, 0:8], T.SCB, 0)
+    ts(T.LO[:], q_, 8.0, OP.is_lt)
     need("v", b)
     c_b1 = pick(T.LB[:, 8:16], T.SCB, 1)
-    need("v", c_b0, s_q1)
-    c_h = vcopy(T.HM[:, 0:128], qm(1).indirect(T.LB[:, 0:8]))
-    need("s", c_b1, s_q3)
-    s_h = scopy(T.HM[:, 128:256], qm(3).indirect(T.LB[:, 8:16]))
+    ts(T.HI[:], q_, 8.0, OP.is_ge)
+    c_h = gather("v", T.HM[:, 0:128], T.W[:, 8, :], T.LB[:, 0:8], c_b0, tok[1])
+    last = rank + 1 == NR
+    odd = [lambda: low(0), lambda: low(1), lambda: high(0), lambda: high(1), lambda: small()]
+
+    def small():
+        return ts(T.QI[:], T.IW[:, 0:17:16], q_, OP.add, float(32 * rank), OP.add)
+
+    def row(i):
+        s_tr[i] = ts(T.TR[:, i, :], T.PSD[:, 128:256], T.TM[:, i:i + 1], OP.mult)
+    if last:
+        odd = [lambda: row(2), lambda: row(1)] + odd
+    else:
+        need("s", s_tr[3])
+        for i in (2, 1):
+            s_tr[i] = scopy(T.TR[:, i, :], T.PSD[:, 128:256], scale=T.TM[:, i:i + 1])
+            if i == 2:
+                s_h = gather("s", T.HM[:, 128:256], T.W[:, 24, :], T.LB[:, 8:16], c_b1, tok[3])
+    need("v", dem)
+    odd.pop(0)()
     need("v", c_h)
     a = diag(T.SCC, 0, T.HM[:, 0:128])
+    odd.pop(0)()
     need("v", a)
     c_lc = pick(T.LC[:], T.SCC, 0)
 
     def slot_l(r):
         return T.LL[:, 8 * r:8 * r + 8]
-    if rank + 1 < NR:
-        need("v", c_lc, s_h)
-        c_m = vcopy(T.MM[:], T.HM[:, 128:256].indirect(T.LC[:]))
+    if not last:
+        odd.pop(0)()
+        c_m = gather("v", T.MM[:], T.HM[:, 128:256], T.LC[:], c_lc, s_h)
+        odd.pop(0)()
         need("v", c_m)
         a = diag(T.SCM, 0, T.MM[:])
+        odd.pop(0)()
         need("v", a)
         c_lm = pick(slot_l(rank), T.SCM, 0)
         need("q", c_lm)
         send("e1", later(rank), slot_l(rank), lambda d: slot_l(rank))
+    k_bo1 = where(T.BO1[:], T.ONE[:, 0:128], [[-16, 8], [0, 16]], OP.is_ge, 0, 1)
     iota(T.KC[:, 0:2], [[0, 2]], 0, 128)
     iota(T.KC[:, 2:4], [[128, 2]], 0, 256)
     k_nb = iota(T.NB[:, 8 * rank:8 * rank + 8], [[0, 8]])
+    need("q", k_bo1)
+    k_bo = where(T.BO[:], T.BO1[:], [[16, 8], [0, 16]], OP.is_ge, 15, -1)
+    k_rst = where(T.RST[:], T.ONE[:, 0:32], [[0, 2], [1, 16]], OP.not_equal, 0, 0)
+    need("q", k_bo)
     k_tri = where(T.TRI[:], T.BO[:], [[1, 128]], OP.is_gt, 0, -1)
 
-    scopy(T.RM[:, 0:128], w0(2).indirect(T.LB[:, 0:8]))
-    s_rm = scopy(T.RM[:, 128:256], w0(6).indirect(T.LB[:, 8:16]))
-    s_t1 = scopy(T.T1[:, 128:256], T.PSD[:, 128:256])
-    need("t", s_dg, s_iw, c_q2)
-    for m, win in enumerate((T.IW[:], T.W0[:, 0, 0, :], T.QM[:, 0:4:2, :], T.RM[:])):
-        if m == 3:
-            need("t", s_rm)
-        mm(T.PZ[:, 0:256], T.DG[:, m, :], win, m == 0, False)
-
-    def half(e, m):
-        need(e, s_t1)
-        return (vcopy if e == "v" else scopy)(T.HH[:, m, :], T.T1[:].indirect(lst(m // 2, m % 2, 0)))
-
-    def onto(e, m, i, by, *toks):
-        need(e, *toks)
-        x = (vcopy if e == "v" else scopy)(T.HP[:, m, 128 * i:128 * i + 128],
-                                           T.HH[:, m, 128 * i:128 * i + 128].indirect(by[:, 8 * i:8 * i + 8]))
-        need("t", x)
-        return mm(T.PZ[:, 128 * i:128 * i + 128], T.DG[:, 4 + m, :], T.HP[:, m, 128 * i:128 * i + 128], False, m + i == 3 and m == 2)
-    need("t", k_xb)
-    for u in range(2):
-        for h in range(2):
-            p_x = mm(T.PX[:, 128 * u:128 * u + 128], T.LS[:, u, h, 2:130], T.XB[:, h, :], h == 0, h == 1)
-    s_h3, s_h2 = half("s", 3), half("s", 2)
-    need("v", s_rm)
-    a = [diag(T.SCR, i, T.RM[:, 128 * i:128 * i + 128]) for i in range(2)][1]
-    c_h1 = half("v", 1)
-    need("v", a)
-    c_lr = pick(T.LR[:], T.SCR, 0, 2)
-    c_h0 = half("v", 0)
-    need("t", k_dg, c_h0)
-    mm(T.PZ[:, 0:256], T.DG[:, 4, :], T.HH[:, 0, :], False, False)
+    order = (1, 3, 0, 2)
+    tk = {}
+    for i in (4, 3, 2, 1, 0):
+        for b in order:
+            k = 8 * b + i
+            win = T.TR[:, 3, :] if i == 4 else T.P[:, k + 1, :]
+            if i % 2:
+                need("v", tk[b], s_tr[(i + 1) // 2])
+                tk[b] = tt(T.P[:, k, :], win.indirect(lst(k)), T.TR[:, (i + 1) // 2, :], OP.add)
+            else:
+                tk[b] = gather("v" if i + b % 2 == 0 else "s", T.P[:, k, :], win, lst(k), s_tr[3] if i == 4 else tk[b])
+    pz = (T.PSD[:, 256:384], T.PZ[:, 0:128])
+    need("t", s_dg, c_b1, s_tr[1])
     for i in range(2):
-        onto("s", 3, i, T.LR, s_h3, c_lr)
-        onto("v", 1, i, T.LA, c_h1)
-    onto("s", 2, 0, T.LB, s_h2)
-    p_z = onto("v", 2, 1, T.LB, s_h2)
-    need("s", p_x)
-    s_xw = scopy(T.XW[:], T.PX[:, 0:256])
-    need("s", p_z)
-    scopy(T.ZH[:], T.PZ[:, 128:256], scale=T.HI[:])
-    s_zl = scopy(T.ZL[:], T.PZ[:, 0:128], scale=T.LO[:])
-    need("v", dem)
-    a = ts(T.EI0[:], T.EM[:], 63, OP.bitwise_and)
-    ts(T.EB[:, :, 1, :], T.EM[:], 1.0 / 4096.0, OP.mult, (160.0 - 31.5 / 64.0) / 64.0, OP.add)
-    need("v", a)
-    c_eb = ts(T.EB[:, :, 0, :], T.EI0[:], 1.0 / 64.0, OP.mult, 2.5, OP.add)
-    need("v", s_zl, c_lc)
-    c_pw = tt(T.PW[:], T.ZH[:].indirect(T.LC[:]), T.ZL[:], OP.add)
-    need("t", c_eb)
-    for u in range(2):
-        for h in range(2):
-            p_e = mm(T.PE0[:, 256 * u:256 * u + 256], T.LS[:, u, h, 2:130], T.EB[:, h], h == 0, h == 1)
+        mm(pz[i], T.DG[:, 0, :], xr, True, False)
+        mm(pz[i], T.DG[:, 1, :], T.W[:, 16 * i, :], False, False)
+    p_z = []
+    for i in range(2):
+        a = gather("s", T.PB[:, i, :], T.P[:, 16 * i + 8, :], T.LB[:, 8 * i:8 * i + 8], tk[2 * i + 1])
+        need("t", tk[2 * i])
+        mm(pz[i], T.DG[:, 2, :], T.P[:, 16 * i, :], False, False)
+        need("t", a)
+        p_z.append(mm(pz[i], T.DG[:, 3, :], T.PB[:, i, :], False, True))
 
-    xr = T.IW[:, 0:128]
+    def lower(h):
+        return ts(T.EB[:, h, 0, :], T.EI0[:, h, :], 1.0 / 64.0, OP.mult, 2.5, OP.add)
 
-    def fold(e, ranks, win):
-        c = None
+    def numbers(made):
+        need("t", made)
+        for u in range(2):
+            for h in range(2):
+                x = mm(T.PE0[:, 256 * u:256 * u + 256], T.LS[:, u, h, 2:130], T.EB[:, h], h == 0, h == 1)
+        return x
+    if last:
+        odd.pop(0)()
+        odd.pop(0)()
+    else:
+        lower(0)
+        p_e = numbers(lower(1))
+
+    def fold(e, ranks, win, c):
         for i in ranks:
-            need(e, arrive("e1", i))
             o = T.FB[:, 128 * i:128 * i + 128]
-            c = (vcopy if e == "v" else scopy)(o, win.indirect(slot_l(i)))
-            need(e, c)
+            c = gather(e, o, win, slot_l(i), arrive("e1", i), c)
             win = o
         return win, c
+    lists = list(range(rank - 1, 0, -1))
+    nv = min(3, max(1, len(lists) - 1))
+    if not last:
+        part, c = fold("s", lists[nv:], xr, c_xr)
+    need("s", p_x)
+    s_xw = scopy(T.XW[:], T.PX[:, 0:256])
+    before = [] if last else lists
+    win, b = xr, c_xr
+    for i, (z, by) in enumerate(((T.ZL, T.LO), (T.ZH, T.HI))):
+        win, b = fold("v", before[:nv][i:i + 1], win, b)
+        need("v", p_z[i])
+        c_z = ts(z[:], pz[i], by[:], OP.mult)
+        if last:
+            odd.pop(0)()
+    by, a = T.LL[:, 0:1], arrive("e1", 0) if rank else c_z
+    win, b = fold("v", before[:nv][2:], win, b)
+    if lists[nv:] and not last:
+        by, a = T.X4[:, 0:1], gather("v", T.X4[:], part, by, a, c)
+    need("v", c_z, c_lc)
+    c_pw = tt(T.PW[:], T.ZH[:].indirect(T.LC[:]), T.ZL[:], OP.add)
+    end = T.PW[:]
 
-    def look(out, win, by, *toks):
-        need("v", *toks)
-        return vcopy(out, win.indirect(by))
-    need("v", c_pw)
-    if rank == 0:
-        st = vcopy(T.S0[:, 0:1], T.PW[:, 0:1])
+    def first():
+        need("v", p_t)
+        return vcopy(T.T0[:], T.PT[:, 0:128])
+    if last:
+        end, c_pw = fold("s", lists[:nv], end, c_pw)
+        lower(0)
+        part, c = fold("v", lists[3:4], xr, c_xr)
+        p_e = numbers(lower(1))
+        part, c = fold("v", lists[4:5], part, c)
+        c_t0 = first()
+        part, c = fold("v", lists[5:6], part, c)
+        odd.pop(0)()
+        by, a = T.X4[:, 0:1], gather("v", T.X4[:], part, by, a, c)
     else:
-        by = T.LL[:, 0:1]
-        far = list(range(mine[0] - 1, 0, -1))
-        if first:
-            win, c = fold("v", list(range(rank - 1, 0, -1)), T.PW[:])
-            a = arrive("e1", 0)
-        elif j == 0:
-            low, c = fold("s", far[-1:], xr)
-            win, _ = fold("v", far[:-1], T.PW[:])
-            a = look(T.X4[:], low, by, arrive("e1", 0), c)
-            by = T.X4[:, 0:1]
-        else:
-            own = list(range(rank - 1, mine[0] - 1, -1))
-            few = len(own) < len(far)
-            mid, c = fold("s", far[:-1] if few else far, xr)
-            win, _ = fold("v", own, T.PW[:])
-            a = arrive("e1", 0)
-            if few:
-                low, _ = fold("v", far[-1:], xr)
-                a = look(T.X1[:], low, by, a)
-                by = T.X1[:, 0:1]
-            a = look(T.X4[:], mid, by, a, c)
-            by = T.X4[:, 0:1]
-        st = look(T.S0[:], win, by, a)
+        if lists:
+            by, a = T.X1[:, 0:1], gather("v", T.X1[:], win, by, a, b)
+        c_t0 = first()
+    if rank:
+        st = gather("v", T.OFX[:], end, by, a, c_pw)
+    else:
+        need("v", c_pw)
+        st = ts(T.OFX[:, 0:2], T.FL[:, 64:66], T.PW[:, 0:1], OP.add)
     need("s", p_e)
     s_ew = scopy(T.EW[:], T.PE0[:], scale=64.0, bias=-159.0)
-    need("v", p_t, st, k_nb)
-    a = ts(T.TA[:], T.PT[:, 0, :], T.S0[:, 0:1], OP.subtract)
-    ts(T.OFX[:, 0:2], T.KB[:, 0:2], T.S0[:, 0:1], OP.add, 1.0 / 512.0, OP.mult)
+    a = gather("v", T.TA[:], T.T0[:], T.OFX[:, 0:1], st, c_t0, k_nb)
+    vcopy(T.OFP[:, 0:1], T.OFX[:, 0:1])
+    b = ts(T.OFP[:, 1:2], T.OFX[:, 0:1], 128.0, OP.add)
+    if rank == 1:
+        b = vcopy(T.OFX[:, 1:2], T.OFX[:, 0:1])
+        need("v", b)
     need("v", a)
-    a = reduce_(T.RA[:], T.TA[:], OP.min, apply_absolute_value=True)
-    ts(T.OFP[:, 0:2], T.KB[:, 2:4], T.S0[:, 0:1], OP.add, 1.0 / 512.0, OP.mult)
+    a = scan(T.RA[:], T.SD[:, 0:16], T.TA[:], OP.add, OP.max)
+
+    def flags(u):
+        return tt(T.FL[:, 32 * u:32 * u + 32], T.XW[:].indirect(T.OFX[:, 2 * u:2 * u + 2]), T.MKI[:, 0:32], OP.is_gt)
+
+    def values(u):
+        return tt(T.GV[:, 32 * u:32 * u + 32], T.EW[:].indirect(T.OFP[:, 2 * u:2 * u + 2]), T.FL[:, 32 * u:32 * u + 32],
+                  OP.mult)
+    need("v", s_xw, s_mk)
+    c = flags(0)
     need("v", a)
-    a = ts(T.OFX[:, 2:4], T.KC[:, 0:2], T.RA[:], OP.add)
-    c_of = ts(T.OFP[:, 2:4], T.KC[:, 2:4], T.RA[:], OP.add)
-    need("v", a, s_xw, s_mk)
-    a = tt(T.FL[:, 0:64], T.XW[:].indirect(T.OFX[:]), T.MKI[:], OP.is_gt)
+    a = ts(T.OFX[:, 2:4], T.KC[:, 0:2], T.RA[:, 15:16], OP.add, T.CORR[:], OP.add)
+    c_of = ts(T.OFP[:, 2:4], T.KC[:, 2:4], T.RA[:, 15:16], OP.add, T.CORR[:], OP.add)
+    need("v", a)
+    a = flags(1)
+    need("v", b, c, s_ew)
+    b = values(0)
     need("v", a)
     c_inc = scan(T.INC[:], T.ONE[:, 0:68], T.FL[:], OP.mult, OP.add)
-    need("v", c_of, s_ew)
-    c_gv = tt(T.GV[:], T.EW[:].indirect(T.OFP[:]), T.FL[:, 0:64], OP.mult)
+    need("v", c_of)
+    c_gv = values(1)
     need("t", c_inc, k_tri)
+    if not last:
+        p_n = mm(T.PN[:, 0:1], T.BO[:], T.INC[:, 64:65])
     mm(T.PSO[:, 0:4], T.TRI[:], T.INC[:, 64:68], True, False)
     p_b = mm(T.PSO[:, 0:4], T.ID[:], T.INC[:, 15:64:16], False, True)
-    p_n = mm(T.PN[:, 0:1], T.BO[:], T.INC[:, 64:65])
-    need("v", k_rst, c_gv)
-    c_scn = scan(T.SCN[:], T.RST[:], T.GV[:], OP.mult, OP.add)
+    if last:
+        p_n = mm(T.PN[:, 0:1], T.BO[:], T.INC[:, 64:65])
+    c_scn = []
+    for u, x in enumerate((b, c_gv)):
+        need("v", k_rst, x)
+        c_scn.append(scan(T.SCN[:, 32 * u:32 * u + 32], T.RST[:], T.GV[:, 32 * u:32 * u + 32], OP.mult, OP.add))
     need("s", p_n, k_nb)
     s_n = scopy(T.NB[:, 8 * rank:8 * rank + 1], T.PN[:, 0:1])
     s_own = scopy(T.OWN[:], T.PN[:, 0:1])
@@ -433,9 +437,9 @@ def rank_program(g, core, T, topo):
     if rank + 1 < NR:
         need("q", s_n)
         send("en", later(rank), T.NB[:, 8 * rank:8 * rank + 8], lambda d: T.NB[:, 8 * rank:8 * rank + 8])
-    need("v", p_b, c_scn)
     need("t", c_ofs)
     for i in range(4):
+        need("v", p_b, c_scn[i // 2])
         a = ts(T.OH[:, i, :], T.IW[:, 1:65], T.PSO[:, i:i + 1], OP.is_equal, T.SCN[:, 16 * i + 15:16 * i + 16], OP.mult)
         need("t", a)
         p_a = mm(T.PSA[:, 256:320], T.BO[:], T.OH[:, i, :], i == 0, i == 3)
@@ -443,40 +447,36 @@ def rank_program(g, core, T, topo):
     hi = 192 if rank + 2 < NR else 144 if rank + 1 < NR else 128
     c_ql = ts(T.QL[:], T.QI[:], float(64 - lo), OP.add)
     need("v", s_own)
-    c_qo = ts(T.QO[:], T.QI[:], T.OWN[:], OP.subtract)
+    c_qo = ts(T.QO[:], T.QI[:, 1:2], T.OWN[:], OP.subtract)
     need("v", p_a)
     c_a = ts(T.F[:, 64:128], T.PSA[:, 256:320], -1.0, OP.add)
     need("q", c_a)
     n = 64 if rank + 1 < NR else 16
     send("ev", beside(rank), T.F[:, 64:64 + n], lambda d: T.F[:, 0:n] if d > rank else T.F[:, 128:128 + n])
 
-    parts = [T.QL]
     beg = 0.0
     need("v", s_b1, c_qo)
     if rank > 0:
+        need("v", arrive("en", rank - 1))
+        c = ts(T.A1[:], T.NB[:, 8 * rank - 8:8 * rank - 7], 64.0, OP.subtract)
         for i in range(rank):
             need("v", arrive("en", i))
-        b = reduce_(T.BEG[:], T.NB[:, 0:8 * rank - 7:8], OP.add)
-        c = ts(T.A1[:], T.NB[:, 8 * rank - 8:8 * rank - 7], 64.0, OP.subtract)
-        need("v", b)
+        need("v", reduce_(T.BEG[:], T.NB[:, 0:8 * rank - 7:8], OP.add))
         beg = T.BEG[:]
-        ts(T.U[:], T.QL[:], beg, OP.subtract)
-        parts = [T.U]
-    if rank + 1 < NR:
-        a = ts(T.U1[:], T.QO[:], beg, OP.is_ge, T.B1[:], OP.mult)
-        parts.append(T.U1)
+    jump = {}
     if rank > 0:
-        need("v", c)
-        a = ts(T.U3[:], T.QI[:], beg, OP.is_lt, T.A1[:], OP.mult)
-        parts.append(T.U3)
-    need("v", a)
-    for i in range(2):
-        x = [p[:, i:i + 1] for p in parts]
-        a = ts(T.OF2[:, i:i + 1], x[0], x[1], OP.add, *((x[2], OP.add) if len(x) > 2 else ()))
+        jump[0] = ts(T.U[:, 0:1], T.QI[:, 0:1], beg, OP.is_lt, T.A1[:], OP.mult)
+    if not last:
+        jump[1] = ts(T.U[:, 1:2], T.QO[:], beg, OP.is_ge, T.B1[:], OP.mult)
+    for i in sorted(range(2), key=lambda i: i in jump):
+        if i in jump:
+            need("v", jump[i])
+            a = ts(T.OF2[:, i:i + 1], T.U[:, i:i + 1], T.QL[:, i:i + 1], OP.add, beg, OP.subtract)
+        else:
+            a = ts(T.OF2[:, i:i + 1], T.QL[:, i:i + 1], beg, OP.subtract)
     for i in beside(rank):
         need("v", arrive("ev", i))
-    need("v", a, c_a)
-    a = vcopy(T.Y1[:], T.F[:, lo:hi].indirect(T.OF2[:]))
+    a = gather("v", T.Y1[:], T.F[:, lo:hi], T.OF2[:], a, c_a)
     need("y", a)
     g.sync.dma_start(T.y[:, :], T.Y1[0:128:16, :]).then_inc(T.sem.dy, 16)
     need("y", ("dy", 16))

from concourse.bass import DstId, RemoteDMATransfer
from concourse.mybir import dt, AluOpType, AxisListType, ActivationFunctionType

_BUF = {
    "int32": "PI:1 CI:4 SYH:16 SYN:2 X:2x128 XA:2x128 EM:2x128 EI0:2x128",
    "uint16": "OFS:16 LST:256 LB:16 LC:8 LL:64 X1:16 X4:16 OFX:16 OFP:4 OF2:2",
    "float32": "CF:4 MS:4 TM:4 CORR:1 SYF:2 LO:1 HI:1 KC:4 RA:16 OWN:1 BEG:1 A1:1 B1:1 QI:2 QO:1 QL:2 U:2 Y1:32 SCN:64",
    "bfloat16": "ONE:130 IW:128 ID:128 IS:128 R:128 J16:144 SD0:144 SD:128 DG:4x128 T0:128 TA:16 MKI:64 BO1:128 BO:128 "
                "TRI:128 RST:32 SYB:16 XI:8x2x16 TL:256 ST:64 SEL:2x2x16 LS:2x2x130 W:32x128 SCB:256 SCC:128 SCM:128 "
                "HM:256 MM:128 TR:4x128 P:32x128 PB:2x128 ZL:128 ZH:128 PW:128 FB:896 "
                "XB:2x128 XW:256 EB:2x2x128 EW:512 GV:64 FL:68 INC:68 OH:4x64 NB:64 F:192",
}
SCRATCH = {n: ("sbuf", [128] + [int(x) for x in d.split("x")], t)
           for t, l in _BUF.items() for n, d in (w.split(":") for w in l.split())}
for _n, _d in (("PSA", [512]), ("PSD", [512]), ("PZ", [512]), ("PT", [512]), ("PE0", [512]), ("PSO", [512]),
               ("PN", [512]), ("PX", [512])):
    SCRATCH[_n] = ("psum", [128] + _d, "float32")
SEMAPHORES = (["v", "s", "t", "q", "dsh", "dsn", "dx0", "dx1", "dem", "dy", "ls"]
              + [p + "_%d" % j for p in ("e1", "en", "ev") for j in range(8)])


def rank_program(g, core, T, topo):
    rank = T.rank_of(core)
    if rank is None:
        return
    OP, ACT, AX = AluOpType, ActivationFunctionType, AxisListType
    NR = len(T.cores)
    mine = [r for r, c in enumerate(T.cores) if topo.chip(c) == topo.chip(core)]
    j = mine.index(rank)
    Q = {"v": g.vector, "s": g.scalar, "t": g.tensor, "q": g, "y": g.sync}
    cnt = {"v": 0, "s": 0, "t": 0, "q": 0}
    seen = {}
    V, S, PE = g.vector, g.scalar, g.tensor

    def need(e, *toks):
        for sem, n in toks:
            if seen.get((e, sem), 0) < n:
                Q[e].wait_ge(T.sem[sem], n)
                seen[(e, sem)] = n

    def did(e, ins):
        cnt[e] += 1
        ins.then_inc(T.sem[e], 1)
        return (e, cnt[e])

    def ts(out, in0, s1, op0, s2=None, op1=None):
        if op1 is None:
            return did("v", V.tensor_scalar(out, in0, s1, None, op0))
        return did("v", V.tensor_scalar(out, in0, s1, s2, op0, op1))

    def tt(out, in0, in1, op):
        return did("v", V.tensor_tensor(out, in0, in1, op))

    def vcopy(out, in_):
        return did("v", V.tensor_copy(out, in_))

    def fill(ap, x):
        return did("v", V.memset(ap, x))

    def scan(out, d0, d1, o0, o1, init=0.0):
        return did("v", V.tensor_tensor_scan(out, d0, d1, init, o0, o1))

    def reduce_(out, in_, op, **k):
        return did("v", V.tensor_reduce(out, in_, AX.X, op, **k))

    def act(out, in_, func, **k):
        return did("s", S.activation(out, in_, func, **k))

    def scopy(out, in_, **k):
        return act(out, in_, ACT.Copy, **k)

    def gather(e, out, win, by, *toks):
        need(e, *toks)
        return (vcopy if e == "v" else scopy)(out, win.indirect(by))

    def mm(out, lhsT, rhs, start=True, stop=True):
        return did("t", PE.matmul(out, lhsT, rhs, start, stop))

    def iota(out, pattern, cm=0, base=0):
        return did("q", g.iota(out, pattern, base, cm, allow_small_or_imprecise_dtypes=True))

    def where(out, in_, pattern, op, base, cm):
        return did("q", g.affine_select(out, in_, pattern, op, 0.0, base, cm))

    def same(r, r2):
        return topo.chip(T.cores[r]) == topo.chip(T.cores[r2])

    def plan(kind, r, dsts):
        near, far = [d for d in dsts if same(r, d)], [d for d in dsts if not same(r, d)]
        p = []
        if near:
            es = topo.engines(T.cores[r], T.cores[near[0]])
            out = topo.engines(T.cores[r], T.cores[[d for d in range(NR) if not same(r, d)][0]])
            if far or r + 1 == NR:
                es = [e for e in es if e not in out]
            p.append((near, es))
        if kind == "e1":
            near.sort()
            far = [sorted(far)[(r + k) % len(far)] for k in range(len(far))]
        if kind == "en":
            far.sort()
        if far:
            p.append((far, topo.engines(T.cores[r], T.cores[far[0]])))
        return p

    def later(r):
        return list(range(NR - 1, r, -1))

    def beside(r):
        return [x for x in range(NR) if abs(x - r) == 1]

    def arrive(kind, r):
        dsts = beside(r) if kind == "ev" else later(r)
        return ("%s_%d" % (kind, r), [len(es) for ds, es in plan(kind, r, dsts) if rank in ds][0])
    sent = [0]

    def send(kind, dsts, src_, at):
        trs = []
        for ds, es in plan(kind, rank, dsts):
            adr = [topo.addr(T.cores[d]) for d in ds]
            trs.append(RemoteDMATransfer(dst_ids=[DstId(rid=x[0], pnc=x[1]) for x in adr],
                                         dma_engine_mask=sum(1 << e for e in es),
                                         remote_sem=T.sem["%s_%d" % (kind, rank)], srcs=[src_], dsts=[at(d) for d in ds]))
            sent[0] += len(es)
        g.remote_dma_fused(trs, local_sem=T.sem.ls)

    g.sync.dma_start(T.X[:, 0, :], T.nx[0:8:2, :]).then_inc(T.sem.dx0, 16)
    S.dma_start(T.SYH[0:16, :], T.sy[:, :]).then_inc(T.sem.dsh, 16)
    S.dma_start(T.X[:, 1, :], T.nx[1:8:2, :]).then_inc(T.sem.dx1, 16)
    S.dma_start(T.SYN[:], T.sy[:, :]).then_inc(T.sem.dsn, 16)
    dsh, dsn, dx, dem = ("dsh", 16), ("dsn", 16), [("dx0", 16), ("dx1", 16)], ("dem", 32)
    need("y", dx[1])
    g.sync.dma_start(T.EM[:, 0, :], T.em[0:8:2, :]).then_inc(T.sem.dem, 16)
    g.sync.dma_start(T.EM[:, 1, :], T.em[1:8:2, :]).then_inc(T.sem.dem, 16)

    c_one = fill(T.ONE[:], 1.0)
    k_pi = did("q", g.iota(T.PI[:], [[0, 1]], 0, 32))
    need("q", c_one)
    k_r = where(T.R[0:16, :], T.ONE[0:16, 0:128], [[1, 16], [0, 8]], OP.is_equal, 0, -1)
    k_j16 = iota(T.J16[:], [[0, 9], [1, 16]])
    k_id = where(T.ID[:], T.ONE[:, 0:128], [[-1, 128]], OP.is_equal, 0, 1)

    need("v", c_one)
    c_xr = scan(T.IW[:, 0:128], T.ONE[:, 0:128], T.ONE[:, 0:128], OP.mult, OP.add, -1.0)
    xr = T.IW[:, 0:128]
    need("v", k_pi)
    for i, (sh, m) in enumerate(((5, 15), (0, 255), (5, 7), (5, 3))):
        a = ts(T.CI[:, i:i + 1], T.PI[:], sh, OP.arith_shift_right, m, OP.bitwise_and)
    need("v", a)
    c_cf = vcopy(T.CF[:], T.CI[:])
    q_, c32, q8, q4 = [T.CF[:, i:i + 1] for i in range(4)]
    c_fl = fill(T.FL[:, 64:68], 0.0)
    need("v", c_cf, c_xr)
    ts(T.MS[:, 0:2], T.IW[:, 0:8:4], q8, OP.is_equal)
    ts(T.MS[:, 2:3], q8, 4.0, OP.is_lt)
    c_ms = ts(T.MS[:, 3:4], q8, 4.0, OP.is_ge)
    ts(T.CORR[:], q_, 15.0, OP.is_lt, -128.0, OP.mult)
    ts(T.TM[:], T.IW[:, 0:4], q4, OP.is_equal)

    need("s", c_one, c_xr)
    for u in range(2):
        for h in range(2):
            s_z = scopy(T.LS[:, u, h, :], T.ONE[:], scale=0.0)
    need("s", k_id, c_ms)
    s_is = scopy(T.IS[:], T.ID[:], scale=-1.0 / 512.0)
    for m in range(4):
        s_dg = scopy(T.DG[:, m, :], T.ID[:], scale=T.MS[:, m:m + 1])

    need("v", dsh)
    c_syb = vcopy(T.SYB[0:16, :], T.SYH[0:16, :])
    need("t", c_syb, k_r)
    p_of = mm(T.PSA[:, 0:16], T.R[0:16, :], T.SYB[0:16, :])
    c_a = []
    for h in range(2):
        need("v", dx[h])
        c_a.append(ts(T.XA[:, h, :], T.X[:, h, :], 127, OP.bitwise_and))
        if h == 0:
            need("v", k_j16)
            c_sd0 = ts(T.SD0[:], T.J16[:], q_, OP.is_equal, -65536.0, OP.mult)
    for h in range(2):
        need("v", c_a[h])
        c_xi = vcopy(T.XI[:, :, h, :], T.XA[:, h, :])
    need("v", p_of)
    c_ofs = ts(T.OFS[:], T.PSA[:, 0:16], c32, OP.add)
    need("v", dsn)
    c_syf = vcopy(T.SYF[:], T.SYN[:])
    need("v", c_xi)
    c_tl = did("v", V.transpose(T.TL[:], T.XI[:]))
    need("v", c_syf)
    for u in range(2):
        c_st = ts(T.ST[:, 32 * u:32 * u + 32], T.IW[:, 0:32], T.SYF[:, u:u + 1], OP.is_equal)
    c_l = {e: gather("v", T.LST[:, 128 * e:128 * e + 128], T.TL[:], T.OFS[:, 8 * e:8 * e + 8], c_tl, c_ofs) for e in (0, 1)}
    need("v", c_st)
    c_sel = did("v", V.transpose(T.SEL[:], T.ST[:]))

    need("q", c_sel, s_z)
    for a in range(4):
        need("q", ("q", cnt["q"]))
        for h in range(2):
            o = 2 + 32 * a + 16 * h
            k_ls = where(T.LS[32 * a:32 * a + 32, :, h, o:o + 16], T.SEL[32 * a:32 * a + 32, :, h, :], [[0, 32]],
                         OP.is_equal, 0, 0)
    need("q", k_ls, *dx)
    k_xb = where(T.XB[:], T.X[:], [[0, 256]], OP.is_equal, 0, 0)
    need("t", c_sd0, k_id, s_is)
    mm(T.PSD[:, 0:128], T.ID[:], T.SD0[:, 16:144], True, False)
    p_sd = mm(T.PSD[:, 0:128], T.IS[:], T.SD0[:, 15:143], False, True)
    need("s", p_sd)
    s_sd = scopy(T.SD[:], T.PSD[:, 0:128])
    for i in range(2):
        s_mk = scopy(T.MKI[:, 16 * i:16 * i + 16], T.SD0[:, 0:16], scale=1.0 / 64.0, bias=1151.0 + 128.0 * i)
    need("t", k_ls, c_xi, s_sd)
    for h in range(2):
        p_t1 = mm(T.PSD[:, 128:256], T.LS[:, 1, h, 1:129], T.XI[:, :, h, :], h == 0, h == 1)
    for h in range(2):
        p_t = mm(T.PT[:, 0:128], T.LS[:, 0, h, 2:130], T.XI[:, :, h, :], h == 0, h == 1)
    need("t", k_xb)
    for u in range(2):
        for h in range(2):
            p_x = mm(T.PX[:, 128 * u:128 * u + 128], T.LS[:, u, h, 2:130], T.XB[:, h, :], h == 0, h == 1)

    def lst(k):
        o = 16 * (k % 16) + 8 * (k // 16)
        return T.LST[:, o:o + 8]
    tok = {0: c_l[0], 1: c_l[1], 2: c_l[0], 3: c_l[1]}
    for i in range(7, -1, -1):
        for b in range(4):
            k = 8 * b + i
            tok[b] = gather("s" if k == 7 else "vs"[b % 2], T.W[:, k, :], xr if i == 7 else T.W[:, k + 1, :], lst(k), tok[b])

    def diag(sc, at, win):
        return scan(sc[:, 128 * at:128 * at + 128], T.SD[:], win, OP.add, OP.max)

    def pick(out, sc, at):
        return ts(out, sc[:, 128 * at + 15:128 * at + 128:16], T.CORR[:], OP.add)

    def low(h):
        return ts(T.EI0[:, h, :], T.EM[:, h, :], 63, OP.bitwise_and)

    def high(h):
        return ts(T.EB[:, h, 1, :], T.EM[:, h, :], 1.0 / 4096.0, OP.mult, (160.0 - 31.5 / 64.0) / 64.0, OP.add)
    need("v", tok[0], s_sd)
    a = diag(T.SCB, 0, T.W[:, 0, :])
    need("v", p_t1)
    s_tr = {3: ts(T.TR[:, 3, :], T.PSD[:, 128:256], T.TM[:, 3:4], OP.mult)}
    need("v", tok[2])
    b = diag(T.SCB, 1, T.W[:, 16, :])
    need("v", a)
    c_b0 = pick(T.LB[:, 0:8], T.SCB, 0)
    ts(T.LO[:], q_, 8.0, OP.is_lt)
    need("v", b)
    c_b1 = pick(T.LB[:, 8:16], T.SCB, 1)
    ts(T.HI[:], q_, 8.0, OP.is_ge)
    c_h = gather("v", T.HM[:, 0:128], T.W[:, 8, :], T.LB[:, 0:8], c_b0, tok[1])
    last = rank + 1 == NR
    odd = [lambda: low(0), lambda: low(1), lambda: high(0), lambda: high(1), lambda: small()]

    def small():
        return ts(T.QI[:], T.IW[:, 0:17:16], q_, OP.add, float(32 * rank), OP.add)

    def row(i):
        s_tr[i] = ts(T.TR[:, i, :], T.PSD[:, 128:256], T.TM[:, i:i + 1], OP.mult)
    if last:
        odd = [lambda: row(2), lambda: row(1)] + odd
    else:
        need("s", s_tr[3])
        for i in (2, 1):
            s_tr[i] = scopy(T.TR[:, i, :], T.PSD[:, 128:256], scale=T.TM[:, i:i + 1])
            if i == 2:
                s_h = gather("s", T.HM[:, 128:256], T.W[:, 24, :], T.LB[:, 8:16], c_b1, tok[3])
    need("v", dem)
    odd.pop(0)()
    need("v", c_h)
    a = diag(T.SCC, 0, T.HM[:, 0:128])
    odd.pop(0)()
    need("v", a)
    c_lc = pick(T.LC[:], T.SCC, 0)

    def slot_l(r):
        return T.LL[:, 8 * r:8 * r + 8]
    if not last:
        odd.pop(0)()
        c_m = gather("v", T.MM[:], T.HM[:, 128:256], T.LC[:], c_lc, s_h)
        odd.pop(0)()
        need("v", c_m)
        a = diag(T.SCM, 0, T.MM[:])
        odd.pop(0)()
        need("v", a)
        c_lm = pick(slot_l(rank), T.SCM, 0)
        need("q", c_lm)
        send("e1", later(rank), slot_l(rank), lambda d: slot_l(rank))
    k_bo1 = where(T.BO1[:], T.ONE[:, 0:128], [[-16, 8], [0, 16]], OP.is_ge, 0, 1)
    iota(T.KC[:, 0:2], [[0, 2]], 0, 128)
    iota(T.KC[:, 2:4], [[128, 2]], 0, 256)
    k_nb = iota(T.NB[:, 8 * rank:8 * rank + 8], [[0, 8]])
    need("q", k_bo1)
    k_bo = where(T.BO[:], T.BO1[:], [[16, 8], [0, 16]], OP.is_ge, 15, -1)
    k_rst = where(T.RST[:], T.ONE[:, 0:32], [[0, 2], [1, 16]], OP.not_equal, 0, 0)
    need("q", k_bo)
    k_tri = where(T.TRI[:], T.BO[:], [[1, 128]], OP.is_gt, 0, -1)

    order = (1, 3, 0, 2)
    tk = {}
    for i in (4, 3, 2, 1, 0):
        for b in order:
            k = 8 * b + i
            win = T.TR[:, 3, :] if i == 4 else T.P[:, k + 1, :]
            if i % 2:
                need("v", tk[b], s_tr[(i + 1) // 2])
                tk[b] = tt(T.P[:, k, :], win.indirect(lst(k)), T.TR[:, (i + 1) // 2, :], OP.add)
            else:
                tk[b] = gather("v" if i + b % 2 == 0 else "s", T.P[:, k, :], win, lst(k), s_tr[3] if i == 4 else tk[b])
    pz = (T.PSD[:, 256:384], T.PZ[:, 0:128])
    need("t", s_dg, c_b1, s_tr[1])
    for i in range(2):
        mm(pz[i], T.DG[:, 0, :], xr, True, False)
        mm(pz[i], T.DG[:, 1, :], T.W[:, 16 * i, :], False, False)
    p_z = []
    for i in range(2):
        a = gather("s", T.PB[:, i, :], T.P[:, 16 * i + 8, :], T.LB[:, 8 * i:8 * i + 8], tk[2 * i + 1])
        need("t", tk[2 * i])
        mm(pz[i], T.DG[:, 2, :], T.P[:, 16 * i, :], False, False)
        need("t", a)
        p_z.append(mm(pz[i], T.DG[:, 3, :], T.PB[:, i, :], False, True))

    def lower(h):
        return ts(T.EB[:, h, 0, :], T.EI0[:, h, :], 1.0 / 64.0, OP.mult, 2.5, OP.add)

    def numbers(made):
        need("t", made)
        for u in range(2):
            for h in range(2):
                x = mm(T.PE0[:, 256 * u:256 * u + 256], T.LS[:, u, h, 2:130], T.EB[:, h], h == 0, h == 1)
        return x
    if last:
        odd.pop(0)()
        odd.pop(0)()
    else:
        lower(0)
        p_e = numbers(lower(1))

    def fold(e, ranks, win, c):
        for i in ranks:
            o = T.FB[:, 128 * i:128 * i + 128]
            c = gather(e, o, win, slot_l(i), arrive("e1", i), c)
            win = o
        return win, c
    lists = list(range(rank - 1, 0, -1))
    nv = min(3, max(1, len(lists) - 1))
    if not last:
        part, c = fold("s", lists[nv:], xr, c_xr)
    need("s", p_x)
    s_xw = scopy(T.XW[:], T.PX[:, 0:256])
    before = [] if last else lists
    win, b = xr, c_xr
    for i, (z, by) in enumerate(((T.ZL, T.LO), (T.ZH, T.HI))):
        win, b = fold("v", before[:nv][i:i + 1], win, b)
        need("v", p_z[i])
        c_z = ts(z[:], pz[i], by[:], OP.mult)
        if last:
            odd.pop(0)()
    by, a = T.LL[:, 0:1], arrive("e1", 0) if rank else c_z
    win, b = fold("v", before[:nv][2:], win, b)
    if lists[nv:] and not last:
        by, a = T.X4[:, 0:1], gather("v", T.X4[:], part, by, a, c)
    need("v", c_z, c_lc)
    c_pw = tt(T.PW[:], T.ZH[:].indirect(T.LC[:]), T.ZL[:], OP.add)
    end = T.PW[:]

    def first():
        need("v", p_t)
        return vcopy(T.T0[:], T.PT[:, 0:128])
    if last:
        end, c_pw = fold("s", lists[:nv], end, c_pw)
        lower(0)
        part, c = fold("v", lists[3:4], xr, c_xr)
        p_e = numbers(lower(1))
        part, c = fold("v", lists[4:5], part, c)
        c_t0 = first()
        part, c = fold("v", lists[5:6], part, c)
        odd.pop(0)()
        by, a = T.X4[:, 0:1], gather("v", T.X4[:], part, by, a, c)
    else:
        if lists:
            by, a = T.X1[:, 0:1], gather("v", T.X1[:], win, by, a, b)
        c_t0 = first()
    if rank:
        st = gather("v", T.OFX[:], end, by, a, c_pw)
    else:
        need("v", c_pw)
        st = ts(T.OFX[:, 0:2], T.FL[:, 64:66], T.PW[:, 0:1], OP.add)
    need("s", p_e)
    s_ew = scopy(T.EW[:], T.PE0[:], scale=64.0, bias=-159.0)
    a = gather("v", T.TA[:], T.T0[:], T.OFX[:, 0:1], st, c_t0, k_nb)
    vcopy(T.OFP[:, 0:1], T.OFX[:, 0:1])
    b = ts(T.OFP[:, 1:2], T.OFX[:, 0:1], 128.0, OP.add)
    if rank == 1:
        b = vcopy(T.OFX[:, 1:2], T.OFX[:, 0:1])
        need("v", b)
    need("v", a)
    a = scan(T.RA[:], T.SD[:, 0:16], T.TA[:], OP.add, OP.max)

    def flags(u):
        return tt(T.FL[:, 32 * u:32 * u + 32], T.XW[:].indirect(T.OFX[:, 2 * u:2 * u + 2]), T.MKI[:, 0:32], OP.is_gt)

    def values(u):
        return tt(T.GV[:, 32 * u:32 * u + 32], T.EW[:].indirect(T.OFP[:, 2 * u:2 * u + 2]), T.FL[:, 32 * u:32 * u + 32],
                  OP.mult)
    need("v", s_xw, s_mk)
    c = flags(0)
    need("v", a)
    a = ts(T.OFX[:, 2:4], T.KC[:, 0:2], T.RA[:, 15:16], OP.add, T.CORR[:], OP.add)
    c_of = ts(T.OFP[:, 2:4], T.KC[:, 2:4], T.RA[:, 15:16], OP.add, T.CORR[:], OP.add)
    need("v", a)
    a = flags(1)
    need("v", b, c, s_ew)
    b = values(0)
    need("v", a)
    c_inc = scan(T.INC[:], T.ONE[:, 0:68], T.FL[:], OP.mult, OP.add)
    need("v", c_of)
    c_gv = values(1)
    need("t", c_inc, k_tri)
    if not last:
        p_n = mm(T.PN[:, 0:1], T.BO[:], T.INC[:, 64:65])
    mm(T.PSO[:, 0:4], T.TRI[:], T.INC[:, 64:68], True, False)
    p_b = mm(T.PSO[:, 0:4], T.ID[:], T.INC[:, 15:64:16], False, True)
    if last:
        p_n = mm(T.PN[:, 0:1], T.BO[:], T.INC[:, 64:65])
    c_scn = []
    for u, x in enumerate((b, c_gv)):
        need("v", k_rst, x)
        c_scn.append(scan(T.SCN[:, 32 * u:32 * u + 32], T.RST[:], T.GV[:, 32 * u:32 * u + 32], OP.mult, OP.add))
    need("s", p_n, k_nb)
    s_n = scopy(T.NB[:, 8 * rank:8 * rank + 1], T.PN[:, 0:1])
    s_own = scopy(T.OWN[:], T.PN[:, 0:1])
    s_b1 = scopy(T.B1[:], T.PN[:, 0:1], scale=-1.0, bias=64.0)
    if rank + 1 < NR:
        need("q", s_n)
        send("en", later(rank), T.NB[:, 8 * rank:8 * rank + 8], lambda d: T.NB[:, 8 * rank:8 * rank + 8])
    need("t", c_ofs)
    for i in range(4):
        need("v", p_b, c_scn[i // 2])
        a = ts(T.OH[:, i, :], T.IW[:, 1:65], T.PSO[:, i:i + 1], OP.is_equal, T.SCN[:, 16 * i + 15:16 * i + 16], OP.mult)
        need("t", a)
        p_a = mm(T.PSA[:, 256:320], T.BO[:], T.OH[:, i, :], i == 0, i == 3)
    lo = 0 if rank > 0 else 64
    hi = 192 if rank + 2 < NR else 144 if rank + 1 < NR else 128
    c_ql = ts(T.QL[:], T.QI[:], float(64 - lo), OP.add)
    need("v", s_own)
    c_qo = ts(T.QO[:], T.QI[:, 1:2], T.OWN[:], OP.subtract)
    need("v", p_a)
    c_a = ts(T.F[:, 64:128], T.PSA[:, 256:320], -1.0, OP.add)
    need("q", c_a)
    n = 64 if rank + 1 < NR else 16
    send("ev", beside(rank), T.F[:, 64:64 + n], lambda d: T.F[:, 0:n] if d > rank else T.F[:, 128:128 + n])

    beg = 0.0
    need("v", s_b1, c_qo)
    if rank > 0:
        need("v", arrive("en", rank - 1))
        c = ts(T.A1[:], T.NB[:, 8 * rank - 8:8 * rank - 7], 64.0, OP.subtract)
        for i in range(rank):
            need("v", arrive("en", i))
        need("v", reduce_(T.BEG[:], T.NB[:, 0:8 * rank - 7:8], OP.add))
        beg = T.BEG[:]
    jump = {}
    if rank > 0:
        jump[0] = ts(T.U[:, 0:1], T.QI[:, 0:1], beg, OP.is_lt, T.A1[:], OP.mult)
    if not last:
        jump[1] = ts(T.U[:, 1:2], T.QO[:], beg, OP.is_ge, T.B1[:], OP.mult)
    for i in sorted(range(2), key=lambda i: i in jump):
        if i in jump:
            need("v", jump[i])
            a = ts(T.OF2[:, i:i + 1], T.U[:, i:i + 1], T.QL[:, i:i + 1], OP.add, beg, OP.subtract)
        else:
            a = ts(T.OF2[:, i:i + 1], T.QL[:, i:i + 1], beg, OP.subtract)
    for i in beside(rank):
        need("v", arrive("ev", i))
    a = gather("v", T.Y1[:], T.F[:, lo:hi], T.OF2[:], a, c_a)
    need("y", a)
    g.sync.dma_start(T.y[:, :], T.Y1[0:128:16, :]).then_inc(T.sem.dy, 16)
    need("y", ("dy", 16))
    for e in ("v", "s", "t", "q"):
        need("q", (e, cnt[e]))
    need("q", ("ls", sent[0]))
